import numpy as np, ml_dtypes
CORES = [36,164,52,180,100,228,116,244]
N = 8
import mx_ref
BF = ml_dtypes.bfloat16
def gcols(t, e):
    v = np.concatenate([t.reshape(8, 16, -1, 4), np.zeros((8, 16, 1, 4), BF)], axis=2)
    return np.ascontiguousarray(np.stack([v[g][:, e[g]] for g in range(8)])).reshape(128, -1)
def tile(rs):
    return np.stack(rs, axis=2).reshape(128, -1).astype(BF)
def pick(q, e):
    c = np.concatenate([q[0].reshape(128, -1, 4), np.zeros((128, 1, 4), np.uint8)], axis=1); s = np.concatenate([q[1], np.ones((16, 1), np.uint8)], axis=1)
    return (np.ascontiguousarray(c[:, e].reshape(128, -1)), np.ascontiguousarray(s[:, e]))
def join(*qs):
    return (np.concatenate([q[0] for q in qs], axis=1), np.concatenate([q[1] for q in qs], axis=1))
def put(q, e, v):
    c, s = q[0].reshape(128, -1, 4).copy(), q[1].copy(); c[:, e] = v[0].reshape(128, -1, 4); s[:, e] = v[1]
    return (c.reshape(128, -1), s)
def pk(c, s):
    return (np.ascontiguousarray(c), mx_ref.live(s))
def emit(q):
    return q[0], q[1]
def packed(v, rng):
    q = [mx_ref.quantize(np.ascontiguousarray(v[r])) for r in range(N)]
    return np.stack([a for a, b in q]), np.stack([mx_ref.plane(b, rng) for a, b in q])
def values_of_codes():
    e, c = np.zeros((128, 128, 4), np.float32), np.zeros((128, 2, 4), np.uint8)
    e[np.arange(128), np.arange(128), 0] = 1
    c[:127, :, 0] = np.arange(256).reshape(2, 128).T[:127]
    return mx_ref.matmul(mx_ref.quantize(e.reshape(128, 512).astype(BF)), (c.reshape(128, 8), np.full((16, 2), 127, np.uint8))).T.reshape(-1).astype(np.float64)
CODE_VALUE, SCALE_VALUE = values_of_codes(), 2.0 ** (np.arange(256) - 127.0)
def decode(q):
    return (CODE_VALUE[q[0]].reshape(16, 8, -1, 4) * SCALE_VALUE[q[1]][:, None, :, None] + 0.0).reshape(128, -1).astype(np.float32)
def f(rng, *shape):
    return mx_ref.flush((rng.standard_normal(shape, dtype=np.float32) * np.exp2(rng.integers(-2, 3, shape[:-1] + (1,)))).astype(BF))
def wide(rng, *shape, cols=0):
    v = rng.standard_normal(shape, dtype=np.float32) * np.exp2(rng.integers(-12, 13, shape)).astype(np.float32)
    if cols: v *= np.repeat(np.exp2(rng.integers(-cols, cols + 1, shape[:-2] + (1, shape[-1] // 4))) * (rng.random(shape[:-2] + (1, shape[-1] // 4)) > 0.0625), 4, axis=-1).astype(np.float32)
    return mx_ref.flush(v.astype(BF))
C, B, K, R = 288, 12, 96, 3
def numbers_of(rng):
    return {"x": np.array(f(rng, N, 128, 4 * C)), "u": np.array(f(rng, N, 128, 512)), "v": np.array(f(rng, N, 128, 512))}
def layers(rng):
    return np.array(f(rng, N, 128, 2048)).reshape(N, 8, 16, 4, 8, 16, 4)
def weights(rng, w):
    c, p = packed(np.ascontiguousarray(w).reshape(N, 128, 2048), rng)
    return {"wc": c, "ws": p}
def lone(u, k, k2=0.0):
    a = u.reshape(N, 128, 128, 4)
    a[:, :, ::16] = 0
    for h in range(0, 128, 16):
        a[:, h, h, 0] = np.asarray(k, np.float32).astype(BF)
        a[:, h + 1, h, 0] = np.asarray(k2, np.float32).astype(BF)
    return a.reshape(N, 128, 512)
def setup_inputs(rng):
    return {**numbers_of(rng), **weights(rng, layers(rng))}
def setup_inputs_ties(rng):
    d = numbers_of(rng)
    m = C // B
    k = (rng.permutation(m) % 5)[:, None]
    one = 1 << rng.integers(0, 8, (N // 2, 2, m, B))
    two = one | (1 << rng.integers(0, 8, one.shape))
    w = np.where(k == 0, one * rng.integers(0, 2, one.shape), np.where(k == 3, two, 0))
    each = 1 << (np.arange(B) % 8)
    w[:, 0] += np.where(k == 2, each, 0)
    w[:, 1] += np.where(k == 4, each, 0)
    w = (w ^ rng.integers(0, 256, 4)[rng.integers(0, 4, (N // 2, 1, m, 1))]).reshape(N, 1, C)
    x = np.zeros((N, 8, 16, C, 4), np.float32)
    x[:, :, 0, :, 0] = ((w >> np.arange(8)[:, None]) & 1) * 2.0 - 1.0
    z = (N, 8, 8, C, 4)
    x[:, :, 8:] = (1.0 + (2 * rng.integers(0, 64, z) + 1) * 2.0 ** -7) * np.exp2(-rng.integers(2, 9, z)) * (rng.integers(0, 2, z) * 2.0 - 1.0)
    x[:, :, 8, :, 0] = 126.0 * (rng.integers(0, 2, (N, 8, C)) * 2.0 - 1.0)
    a = layers(rng)
    a[:, :, :, :, :, :8] = 0
    a[:, :, :, :, rng.permutation(8)[:4]] = 0
    return {"x": x.reshape(N, 128, 4 * C).astype(BF), "u": lone(d["u"], 1.0), "v": d["v"], **weights(rng, a)}
def setup_inputs_near(rng):
    d = numbers_of(rng)
    x = d["x"].reshape(N, 8, 16, C, 4)
    o = np.repeat(rng.permutation(N // 2) % 2, 2)
    small = (o == 0)[:, None, None]
    s = np.where(small, rng.choice([1.125, 2.0, -40.0, -40.0], (N, 8, C)) * 2.0 ** -30, rng.integers(-1, 2, (N, 8, C)))
    less = np.where(small, -1.25 * 2.0 ** -30, np.zeros((N, 8, C)))
    for r in range(N):
        for g in rng.permutation(8)[:4]:
            c = rng.integers(C)
            s[r, g, c] = 2.0 ** 29
            less[r, g, c] = 2.0 ** 29
    x[:, :, :8] = 0
    x[:, :, 0, :, 0] = s.astype(np.float32).astype(BF)
    x[:, :, 1, :, 0] = less.astype(np.float32).astype(BF)
    w = layers(rng)
    w[:, :, :8] = 0
    w[:, :, :, :, :, :8] = 0
    return {"x": x.reshape(N, 128, 4 * C), "u": lone(d["u"], np.where(o == 0, 1.125 * 2.0 ** -30, 1.0), np.where(o == 0, 2.0 ** -30, 1.0)), "v": d["v"], **weights(rng, w)}
def setup_inputs_late(rng):
    d = numbers_of(rng)
    x = d["x"].reshape(N, 8, 16, C, 4)
    p = rng.permutation(N // 2)
    c = rng.choice([-1.0, 1.0]) * (1.0 - 2.0 * (p // 2 % 2))
    s = np.stack([c, np.where(p % 2 == 0, c, -c)], axis=1).reshape(N)
    x[:, :, 0] = s.astype(np.float32).astype(BF)[:, None, None, None]
    z = (N, 8, C, 4)
    a = (1.0 + (2 * rng.integers(0, 64, z) + 1) * 2.0 ** -7) * np.exp2(-rng.integers(13, 15, z))
    a[:, 0, :, 0] = 1.96875
    x[:, 7, 8:] = (a * (rng.integers(0, 2, z) * 2.0 - 1.0)).astype(np.float32).astype(BF)
    x[:, 6, 8:] = 0
    w = layers(rng)
    w[:, :, :, :, 6:, 8:] = 0
    for i in range(8, 16):
        for b in range(4): w[:, 7, i, b, 6, i, b] = 32
    w[:, 7, 8, 0, 6, 8, 0] = 0
    return {"x": x.reshape(N, 128, 4 * C), "u": lone(d["u"], 1.0), "v": d["v"], **weights(rng, w)}
def setup_inputs_ends(rng):
    d = numbers_of(rng)
    x = np.zeros((N, 8, 16, C, 4), np.float32)
    u = d["u"].reshape(N, 8, 16, 128, 4)
    u[:, :, :, ::16] = 0
    w = np.zeros((N, 128, 4, 128, 4), np.float32)
    i = np.arange(128)
    o = rng.permutation(N // 2) % 2
    for p in range(N // 2):
        e = slice(2 * p, 2 * p + 2)
        k = 2.0 ** 30 if o[p] == 0 else 2.0 ** -30
        for g in range(8): u[e, g, :, 16 * g] = k
        if o[p] == 0:
            c = rng.choice([-1.0, 1.0], (C // B, 1)) * np.ones((1, 8))
            h = np.argsort(rng.random(c.shape), axis=1)[:, :2]
            np.put_along_axis(c, h, -c[:, :2], axis=1)
            m = rng.permutation(C // B)[:2]
            c[m[0]], c[m[1]] = 1.0, -1.0
            s = 0.75 + 0.25 * rng.random((2, 8, 16, C, 4))
            for a in m: s[:, :, :, B * a:B * a + B] = 1.0
            x[e] = 2.0 ** 30 * s * np.repeat(c.T, B, axis=1)[:, None, :, None]
            for g in rng.permutation(8)[:4]: u[e, :, :, 16 * g] = k
            d["v"][e] = (2.0 ** 30 * rng.choice([-1.0, 1.0], (2, 128, 512))).astype(np.float32).astype(BF)
            for b in range(4): w[e, i, b, i, b] = -1
        else:
            x[e] = 2.0 ** -30
            for g in range(8): x[2 * p + 1, g][:, np.arange(C) % B % 8 == g] = -7.0 * 2.0 ** -30
    d["v"] = (np.where(d["v"] < 0, -1.0, 1.0) * np.where(rng.permutation(N) % 2, 2.0 ** -30, 2.0 ** 30)[:, None, None]).astype(np.float32).astype(BF)
    return {"x": x.reshape(N, 128, 4 * C).astype(BF), "u": u.reshape(N, 128, 512), "v": d["v"], **weights(rng, w.astype(BF))}
def setup_inputs_spread(rng):
    d = setup_inputs(rng)
    d["x"] = wide(rng, N, 128, 4 * C, cols=6)
    return d
def check_inputs(d):
    b = []
    for k in ("x", "u", "v"):
        a = np.abs(d[k].astype(np.float32))
        if not (np.isfinite(a).all() and ((a == 0) | (a >= 2.0 ** -30) & (a <= 2.0 ** 30)).all()): b.append("a value of " + k)
    none, least, most = [emit(mx_ref.quantize(np.full((128, 16), k, np.float32).astype(BF)))[1][0, 0] for k in (0.0, 2.0 ** -30, 2.0 ** 30)]
    for r in range(N):
        if ((d["wc"][r] == 0x7F) | (d["wc"][r] == 0xFF)).any(): b.append("wc: a code that is no number")
        s = mx_ref.live(d["ws"][r])
        if ((s != none) & ((s < least) | (s > most))).any(): b.append("ws: a scale out of range")
    return b
def reference(x, u, v, wc, ws):
    qu = [mx_ref.quantize(u[r]) for r in range(N)]
    lay = [pk(wc[r], ws[r]) for r in range(N)]
    now = [x[r] for r in range(N)]
    mate = np.arange(N) ^ 1
    after = (np.arange(C)[:, None] + np.arange(1, C)) % C
    for t in range(R):
        q = [mx_ref.quantize(now[r]) for r in range(N)]
        own = [decode(q[r]).astype(BF) for r in range(N)]
        word = np.stack([np.packbits(mx_ref.matmul(qu[r], q[r])[::16] > 0, axis=0, bitorder="little")[0] for r in range(N)])
        theirs = word[:, :, None] ^ np.repeat(word[mate].reshape(N, -1, B), B, axis=1)
        ours = word[:, :, None] ^ word[:, after]
        care = np.full((N, C), 255, np.uint8)
        a, kept = np.zeros((N, 8, C), np.int64), np.zeros((N, 8, C), np.int64)
        for k in range(8):
            g = (3 * t + k) % 8
            bit = np.uint8(1 << g)
            keep = np.any((theirs & care[:, :, None]) == bit, axis=2)
            hit = (ours & care[:, :, None]) == bit
            first = after[np.arange(C), np.argmax(hit, axis=2)]
            a[:, g] = np.where(~keep & np.any(hit, axis=2), first, np.arange(C))
            kept[:, g] = keep
            care = np.where(keep, care, care & np.uint8(255 - (1 << g)))
        l = np.argsort(kept, axis=2, kind="stable")[:, :, :K]
        z = [((own[r].astype(np.float32) + gcols(own[r], a[r]).astype(np.float32)) * np.float32(0.5)).astype(BF) for r in range(N)]
        sent = [mx_ref.quantize(gcols(z[r], l[r])) for r in range(N)]
        now = []
        for r in range(N):
            came = sent[mate[r]]
            held = decode(came)
            made = tile([mx_ref.matmul(pick(lay[r], np.arange(128 * b, 128 * b + 128)), came) * np.float32(0.03125) + held[:, b::4] for b in range(4)]).reshape(8, 16, K, 4)
            new = z[r].reshape(8, 16, C, 4).copy()
            for g in range(8): new[g][:, l[r, g]] = made[g]
            now.append(new.reshape(128, 4 * C))
    y, al = np.zeros((N, 128, C), np.float32), np.zeros((N, 8, C + K), np.float32)
    oc, osc = np.zeros((N, 128, 4 * C), np.uint8), np.zeros((N, 16, C), np.uint8)
    for r in range(N):
        q = mx_ref.quantize(now[r])
        y[r] = mx_ref.matmul(mx_ref.quantize(v[r]), q)
        al[r] = np.concatenate([a[r], l[r]], axis=1)
        oc[r], osc[r] = emit(q)
    return {"y": y, "al": al, "oc": oc, "osc": osc}

@@ -1,0 +1,528 @@
+from concourse.bass import DstId, RemoteDMATransfer
+from concourse.mybir import dt, AluOpType, AxisListType, ActivationFunctionType
+
+N, C, R, NG = 8, 288, 3, 8
+NB = 24
+P = 384
+K = 96
+
+_S = {}
+
+
+def _b(name, cols, dtype, where="sbuf"):
+    _S[name] = (where, [128, cols], dtype)
+
+
+for _n, _c in (("XN", 1152), ("XT", 1536), ("UT", 1024), ("VT", 512), ("FP", 1536), ("FO", 1536), ("TZ", 1920), ("ET", 512), ("BT", 1536), ("DT", 1536),
+               ("EB", 2048), ("TC", 1024), ("CW", 512), ("MC", 1088), ("WR", 384), ("H0", 384), ("H1", 384), ("NEG", 384), ("ONB", 128), ("ID", 128)):
+    _b(_n, _c, "bfloat16")
+for _n, _c in (("XNQ", 288), ("XQ", 384), ("QC", 288), ("UQ", 256), ("VQ", 128), ("EQ", 128), ("LQ", 128), ("BQ", 384), ("DQ", 384),
+               ("EBQ", 512), ("TCQ", 256), ("CWQ", 128), ("MCQ", 272), ("WQ", 512)):
+    _b(_n, _c, "float8_e4m3fn_x4")
+    _b(_n + "S", _c, "uint8")
+for _n, _c in (("SEL8", 8), ("ONE8", 8), ("POW", 24), ("INV", 8), ("IM8", 8), ("T8", 8), ("T8B", 8), ("T8C", 8), ("WP", 1), ("IW", 1), ("IW2", 1), ("WI", 256),
+               ("FLA", 256), ("FLB", 256), ("FLC", 256), ("NBT", 256), ("IP", 2), ("GE", 1), ("PM", 1), ("PMC", 1), ("RC", 1), ("NRC", 1), ("PML", 1), ("QROW", 384),
+               ("MASK", 384), ("PADM", 384), ("NROW", 384), ("IOA", 24), ("IOB", 24), ("IOC", 24), ("NC", 24), ("N96", 24), ("JC", 24), ("PADC", 24),
+               ("PADV", 48), ("BASE", 24), ("O256", 3), ("D0R", 32), ("RM", 32), ("ONE24", 24), ("Z16", 16), ("IOD", 18), ("PLA", 18), ("PLB", 18),
+               ("BJ", 24), ("BW", 24), ("W3", 3), ("W3B", 3), ("XH", 768), ("PA0", 384), ("PA1", 384), ("NX0", 385), ("NX1", 385), ("RIF", 24),
+               ("XG", 48), ("ZZ", 48), ("VV", 48), ("KL", 48), ("MN", 3), ("KEEP", 24), ("KB", 24), ("KU", 24), ("M0", 24), ("M1", 24), ("DROP", 24),
+               ("HI", 1536), ("LO", 384), ("HH", 384), ("RG", 384), ("RMX", 384), ("R1", 192), ("R2", 96), ("R3", 48), ("PR", 24), ("E1", 24), ("EN", 32),
+               ("T1", 32), ("Y3", 96), ("FD0", 32), ("FD", 32), ("L3", 96), ("LA", 24), ("LB", 24), ("LC", 24), ("LD", 24), ("LE", 24), ("LF", 24), ("LG", 24),
+               ("LH", 24), ("LI", 24), ("LK", 24), ("LL", 24), ("LM", 24), ("LN", 24), ("LP", 24), ("LR", 24), ("AA", 24), ("LWW", 384), ("LMK", 96), ("L6", 6),
+               ("AJ", 32), ("AJT", 32), ("YO", 288), ("SC", 384)):
+    _b(_n, _c, "float32")
+for _n, _c in (("DI", 48), ("XK", 384)):
+    _b(_n, _c, "int32")
+for _n, _c in (("WOUT", 4), ("LW0", 4), ("LW1", 4), ("LW2", 4), ("RI", 24), ("AL", 24), ("PL", 24), ("SL", 24), ("L6U", 6), ("PLIN", 24), ("PLOUT", 18)):
+    _b(_n, _c, "uint16")
+_b("PS", 4096, "float32", "psum")
+_SMALL, _WID, _at = {}, {}, 0
+for _n in [n for n in _S if _S[n][2] == "float32" and _S[n][0] == "sbuf" and _S[n][1][1] <= 48 and n not in ("T1", "EN", "MASK")]:
+    _SMALL[_n] = _at
+    _WID[_n] = _S[_n][1][1]
+    _at += -(-_S[_n][1][1] // 16) * 16
+    del _S[_n]
+_OWN = ("SEL8", "ONE8", "POW", "INV", "IM8", "T8", "T8B", "T8C", "WP", "IW", "IW2", "IP")
+_b("FS", _at, "float32")
+_b("FC", _at, "float32")
+SCRATCH = _S
+SEMAPHORES = (["qv", "qa", "qp", "qg"] + ["d%d" % i for i in range(24)]
+              + [n % t for t in range(R) for n in ("wr%d", "wl%d", "er%d", "el%d")])
+_BANKED = {"PS": 512}
+A = AluOpType
+ACT = ActivationFunctionType
+M23 = 1.5 * 2.0 ** 23
+M28 = 1.5 * 2.0 ** 28
+
+
+def rank_program(g, core, T, topo):
+    rank = T.rank_of(core)
+    if rank is None:
+        return
+    mate = T.cores[rank ^ 1]
+    rid, pid = topo.addr(mate, core)
+    mask = topo.mask(core, mate)
+    neng = len(topo.engines(core, mate))
+    Q = {"v": g.vector, "a": g.scalar, "p": g.tensor, "g": g, "s": g.sync}
+    TOK = {"v": "qv", "a": "qa", "p": "qp", "g": "qg"}
+    total = {k: 0 for k in ("qv", "qa", "qp", "qg")}
+    know = {e: {} for e in Q}
+    recs = {}
+    nd = [0]
+
+    def v(name, lo=0, hi=None, st=1, rev=False):
+        if name in _SMALL:
+            buf, o = ("FC" if name in _OWN else "FS"), _SMALL[name]
+            w = _WID[name]
+            return (buf, o + lo, o + (w if hi is None else hi), st, rev)
+        return (name, lo, SCRATCH[name][1][1] if hi is None else hi, st, rev)
+
+    def ap(w):
+        t = T[w[0]]
+        if w[4]:
+            return t[:, w[2] - 1:(w[1] - 1 if w[1] > 0 else None):-1]
+        return t[:, w[1]:w[2]] if w[3] == 1 else t[:, w[1]:w[2]:w[3]]
+
+    def acc(w):
+        if w[0] in _BANKED:
+            return ("%s.%d" % (w[0], w[1] // 512), 0, 1, 1)
+        return w[:4]
+
+    def meet(a, b):
+        if a[1] >= b[2] or b[1] >= a[2]:
+            return False
+        return not (a[3] == b[3] and a[3] > 1 and (a[1] - b[1]) % a[3])
+
+    def sync(e, reads, writes):
+        need = {}
+        me = TOK.get(e)
+        for kind, accs in (("r", reads), ("w", writes)):
+            for x in accs:
+                for (k2, x2, tok, cnt, snap) in recs.get(x[0], ()):
+                    psum = x[0][:3] == "PS."
+                    if kind == "r" and k2 == "r" and not (psum and tok != me):
+                        continue
+                    if tok == me and (psum and me == "qp" or k2 == "r"):
+                        continue
+                    if not meet(x, x2) or know[e].get(tok, 0) >= cnt:
+                        continue
+                    if tok not in need or need[tok][0] < cnt:
+                        need[tok] = (cnt, snap)
+        for tok in sorted(need, key=lambda q: q == me):
+            cnt, snap = need[tok]
+            if know[e].get(tok, 0) >= cnt:
+                continue
+            if any(t2 != tok and s2[1].get(tok, 0) >= cnt for t2, s2 in need.items() if know[e].get(t2, 0) < s2[0]):
+                continue
+            Q[e].wait_ge(T.sem[tok], cnt)
+            for t3, c3 in list(snap.items()) + [(tok, cnt)]:
+                if know[e].get(t3, 0) < c3:
+                    know[e][t3] = c3
+
+    def note(e, reads, writes, tok, cnt):
+        snap = dict(know[e])
+        snap[tok] = cnt
+        for kind, accs in (("r", reads), ("w", writes)):
+            for x in accs:
+                l = recs.setdefault(x[0], [])
+                if kind == "w":
+                    l[:] = [o for o in l if not (x[1] <= o[1][1] and x[2] >= o[1][2] and (x[3] == 1 or (x[3] == o[1][3] and (x[1] - o[1][1]) % x[3] == 0)))]
+                else:
+                    l[:] = [o for o in l if not (o[0] == "r" and o[2] == tok and o[1] == x)]
+                l.append((kind, x, tok, cnt, snap))
+
+    def issue(e, fn, reads, writes):
+        reads, writes = [acc(x) for x in reads], [acc(x) for x in writes]
+        sync(e, reads, writes)
+        tok = TOK[e]
+        total[tok] += 1
+        fn().then_inc(T.sem[tok], 1)
+        note(e, reads, writes, tok, total[tok])
+
+    def dmas(items):
+        tok = "d%d" % nd[0]
+        nd[0] += 1
+        total[tok] = 16 * len(items)
+        for (e, o, i, rd, wr) in items:
+            sync(e, [acc(x) for x in rd], [acc(x) for x in wr if x is not None])
+        for (e, o, i, rd, wr) in items:
+            Q[e].dma_start(o, i).then_inc(T.sem[tok], 16)
+        for (e, o, i, rd, wr) in items:
+            note(e, [acc(x) for x in rd], [acc(x) for x in wr], tok, total[tok])
+
+    def isv(x):
+        return x is not None and not isinstance(x, (int, float))
+
+    def ts(o, i, s1, op0, s2=None, op1=None):
+        a1, a2 = (ap(s1) if isv(s1) else s1), (ap(s2) if isv(s2) else s2)
+        rd = [i] + [x for x in (s1, s2) if isv(x)]
+        if op1 is None:
+            issue("v", lambda: g.vector.tensor_scalar(ap(o), ap(i), a1, None, op0), rd, [o])
+        else:
+            issue("v", lambda: g.vector.tensor_scalar(ap(o), ap(i), a1, a2, op0, op1), rd, [o])
+
+    def tt(o, a, b, op):
+        issue("v", lambda: g.vector.tensor_tensor(ap(o), ap(a), ap(b), op), [a, b], [o])
+
+    def ttg(o, a, off, b, op):
+        issue("v", lambda: g.vector.tensor_tensor(ap(o), ap(a).indirect(ap(off)), ap(b), op), [a, off, b], [o])
+
+    def cp(o, i):
+        issue("v", lambda: g.vector.tensor_copy(ap(o), ap(i)), [i], [o])
+
+    def cpg(o, i, off):
+        issue("v", lambda: g.vector.tensor_copy(ap(o), ap(i).indirect(ap(off))), [i, off], [o])
+
+    def scat(o, off, i):
+        issue("v", lambda: g.vector.tensor_copy(ap(o).indirect(ap(off)), ap(i)), [i, off], [o])
+
+    def pickc(o, i, off):
+        issue("v", lambda: g.vector.tensor_copy(ap(o).bitcast(dt.uint32), ap(i).bitcast(dt.uint32).indirect(ap(off))), [i, off], [o])
+
+    def red(o, i, op):
+        issue("v", lambda: g.vector.tensor_reduce(ap(o), ap(i), AxisListType.X, op), [i], [o])
+
+    def scan(o, a, b, init, op0, op1):
+        ini = ap(init) if isv(init) else init
+        issue("v", lambda: g.vector.tensor_tensor_scan(ap(o), ap(a), ap(b), ini, op0, op1), [a, b] + ([init] if isv(init) else []), [o])
+
+    def tr(o, i):
+        issue("v", lambda: g.vector.transpose(ap(o), ap(i)), [i], [o])
+
+    def ms(o, c):
+        issue("v", lambda: g.vector.memset(ap(o), c), [], [o])
+
+    def qz(q, i, lo=0, hi=None):
+        qv, sv = v(q, lo, hi), v(q + "S", lo, hi)
+        issue("v", lambda: g.vector.quantize_mx(ap(qv), ap(sv), ap(i)), [i], [qv, sv])
+
+    def act(o, i, scale=1.0, off=None):
+        sc = ap(scale) if isv(scale) else scale
+        rd = [i] + ([scale] if isv(scale) else []) + ([off] if off is not None else [])
+        src = (lambda: ap(i).indirect(ap(off))) if off is not None else (lambda: ap(i))
+        if isv(scale) or scale != 1.0:
+            issue("a", lambda: g.scalar.activation(ap(o), src(), ACT.Copy, scale=sc), rd, [o])
+        else:
+            issue("a", lambda: g.scalar.activation(ap(o), src(), ACT.Copy), rd, [o])
+
+    def mm(bank, n, l, ll, r, rl, start=True, stop=True):
+        o = v("PS", 512 * bank, 512 * bank + n)
+        lq, ls, rq, rs = v(l, ll, ll + 128), v(l + "S", ll, ll + 128), v(r, rl, rl + n), v(r + "S", rl, rl + n)
+        issue("p", lambda: g.tensor.matmul_mx(ap(o), ap(lq), ap(ls), ap(rq), ap(rs), start, stop), [lq, ls, rq, rs], [o])
+
+    def iota(o, pat, base=0, ch=0):
+        issue("g", lambda: g.iota(ap(o), pat, base, ch, allow_small_or_imprecise_dtypes=True), [], [o])
+
+    def asel(o, i, pat, op, fill, base, ch):
+        issue("g", lambda: g.affine_select(ap(o), ap(i), pat, op, fill, base, ch), [i], [o])
+
+    def ps(bank, n, lo=0, st=1):
+        return v("PS", 512 * bank + lo, 512 * bank + lo + n, st)
+
+    dmas([("s", T.XN[:, 0:1152], T.x[:, :], [], [v("XN")])])
+    dmas([("a", T.UT[:, 0:512], T.u[:, :], [], [v("UT", 0, 512)]), ("a", T.UT[:, 512:1024], T.u[:, :], [], [v("UT", 512, 1024)])])
+    dmas([("s", T.WQ[:, :].bitcast(dt.uint8), T.wc[:, :], [], [v("WQ")]), ("s", T.WQS[:, :], T.ws[:, :], [], [v("WQS")])])
+    dmas([("s", T.VT[:, :], T.v[:, :], [], [v("VT")])])
+
+    ms(v("ONE8"), 1.0)
+    ms(v("ONB"), 1.0)
+    iota(v("IP", 0, 1), [[0, 1]], 0, 1)
+    asel(v("T8"), v("ONE8"), [[-16, 8]], A.is_ge, 0.0, 0, 1)
+    iota(v("IOA"), [[12, 24]])
+    iota(v("IP", 1, 2), [[0, 1]], 128, 1)
+    asel(v("SEL8"), v("ONE8"), [[-16, 8]], A.is_equal, 0.0, 0, 1)
+    iota(v("WI"), [[1, 256]])
+    asel(v("ID"), v("ONB"), [[-1, 128]], A.is_equal, 0.0, 0, 1)
+    iota(v("QROW"), [[0, 24], [1, 16]])
+    red(v("GE"), v("T8"), A.add)
+    ts(v("PMC"), v("GE"), -16.0, A.mult, 16.0, A.add)
+    tt(v("PM"), v("PMC"), v("IP", 0, 1), A.add)
+    ts(v("PML"), v("PM"), 11.0, A.min)
+    ts(v("PLIN"), v("IOA"), v("PML"), A.add)
+    qz("UQ", v("UT"))
+    qz("XNQ", v("XN"))
+    pickc(v("XQ"), v("XNQ"), v("PLIN"))
+    act(v("XQS"), v("XNQS"), off=v("PLIN"))
+    ms(v("BT"), 0.0)
+    for i in range(8):
+        ms(v("POW", i, 24, 8), 2.0 ** i)
+    iota(v("O256"), [[256, 3]])
+
+    def words(t):
+        u0 = (3 * t % 8) * 16
+        for b in range(3):
+            mm(b, 128, "XQ", 128 * b, "UQ", u0)
+        mm(3, P, "UQ", u0, "XQ", 0)
+        if t:
+            for b in range(4):
+                mm(4 + b, P, "EBQ", 128 * b, "XQ", 0)
+        for b in range(3):
+            ts(v("BJ", 8 * b, 8 * b + 8), ps(b, 128, 0, 16), 0.0, A.is_gt)
+        tt(v("BW"), v("BJ"), v("POW"), A.mult)
+        for b in range(3):
+            red(v("W3", b, b + 1), v("BW", 8 * b, 8 * b + 8), A.add)
+        tt(v("W3B"), v("W3"), v("O256"), A.add)
+        cp(v("WOUT", 0, 3), v("W3B"))
+        lt, rt = "wl%d" % t, "wr%d" % t
+        total[lt] = total[rt] = neng
+        src = v("WOUT", 0, 3)
+        rd = [src]
+        if t == 0:
+            rd = rd + [v("LQ"), v("LQS")]
+        sync("g", rd, [])
+        g.remote_dma(T["LW%d" % t][:, 0:3], T.WOUT[:, 0:3], T.sem[rt], T.sem[lt], pid, rid, mask)
+        note("g", [src], [], lt, neng)
+        recs.setdefault("LW%d" % t, []).append(("w", v("LW%d" % t)[:4], rt, neng, {rt: neng}))
+        ts(v("BT", 0, 1536, 4), ps(3, P), 0.0, A.is_gt)
+        ts(v("BT", 1, 1536, 4), ps(3, P), 0.0, A.is_le)
+        qz("BQ", v("BT"))
+
+    ms(v("ET"), 0.0)
+    qz("LQ", v("ET"))
+    words(0)
+    red_in = v("T8B")
+    issue("v", lambda: g.vector.reciprocal(ap(v("INV")), ap(v("POW", 0, 8))), [v("POW", 0, 8)], [v("INV")])
+    tt(red_in, v("SEL8"), v("POW", 0, 8), A.mult)
+    red(v("WP"), red_in, A.add)
+    tt(v("T8C"), v("SEL8"), v("INV"), A.mult)
+    red(v("IW"), v("T8C"), A.add)
+    ms(v("CW"), 0.0)
+    ts(v("CW", 0, 512, 4), v("ONB"), v("WP"), A.mult)
+    qz("CWQ", v("CW"))
+    mm(3, P, "CWQ", 0, "BQ", 0)
+    asel(v("IM8"), v("INV"), [[-16, 8]], A.is_gt, 0.0, 0, 1)
+    ms(v("MC"), 0.0)
+    ts(v("IW2"), v("IW"), 0.5, A.mult)
+    ts(v("FLA"), v("WI"), v("IW"), A.mult, -0.498, A.add)
+    ts(v("FLB"), v("WI"), v("IW2"), A.mult, -0.498, A.add)
+    ts(v("FLA"), v("FLA"), M23, A.add, M23, A.subtract)
+    ts(v("FLC"), v("FLB"), M23, A.add, M23, A.subtract)
+    ts(v("FLC"), v("FLC"), -2.0, A.mult)
+    tt(v("FLB"), v("FLA"), v("FLC"), A.add)
+    ts(v("NBT"), v("FLB"), -1.0, A.mult, 1.0, A.add)
+    ts(v("MC", 0, 1024, 4), v("NBT"), v("WP"), A.mult)
+    ts(v("MC", 1, 1024, 4), v("FLB"), v("WP"), A.mult)
+    ts(v("MC", 1024, 1056, 4), v("IM8"), v("WP"), A.mult)
+    cp(v("MC", 1025, 1056, 4), v("SEL8"))
+    qz("MCQ", v("MC"))
+    ms(v("EB"), 0.0)
+    for b in range(4):
+        ts(v("EB", 512 * b + b, 512 * b + 512, 4), v("ID"), 32.0, A.mult)
+    qz("EBQ", v("EB"))
+    for b in range(4):
+        mm(4 + b, P, "EBQ", 128 * b, "XQ", 0)
+    ms(v("TC"), 0.0)
+    for e in range(4):
+        cp(v("TC", 512 * (e // 2) + e, 512 * (e // 2) + 512, 4), v("ID"))
+    qz("TCQ", v("TC"))
+    ms(v("NEG"), -1.0)
+    ms(v("DT"), 0.0)
+    ms(v("HI"), 0.0)
+    ms(v("EN"), 0.0)
+    ms(v("Y3"), 0.0)
+    ms(v("AJ"), 0.0)
+    ms(v("Z16"), 0.0)
+    ms(v("ONE24"), 1.0)
+    ms(v("D0R"), 1.0)
+    ms(v("D0R", 0, 32, 16), 0.0)
+    iota(v("NROW"), [[1, P]])
+    iota(v("IOB"), [[16, 24]])
+    iota(v("IOC"), [[4, 24]], 276)
+    for k in range(8):
+        iota(v("BASE", k, 24, 8), [[2 ** (8 - k), 3]], 3 * (512 - 2 ** (9 - k)))
+    iota(v("IOD"), [[16, 18]])
+    ts(v("MASK"), v("QROW"), v("PM"), A.is_equal)
+    ts(v("PADM"), v("QROW"), 12.0, A.is_ge, 1000.0, A.mult)
+    ts(v("PADV"), v("QROW", 0, 48), 12.0, A.is_ge, 1024.0, A.mult)
+    ts(v("RM"), v("QROW", 0, 32), 12.0, A.is_lt)
+    ts(v("RC"), v("PM"), 12.0, A.is_lt)
+    ts(v("NRC"), v("PM"), 12.0, A.is_ge)
+    ts(v("NC"), v("IOB"), v("PM"), A.add)
+    ts(v("N96"), v("NC"), 96.0, A.add)
+    ts(v("JC"), v("IOA"), v("PM"), A.add)
+    ts(v("PADC"), v("IOC"), v("PM"), A.add, v("NRC"), A.mult)
+
+    def seg(k):
+        return 3 * (512 - 2 ** (9 - k))
+
+    for t in range(R):
+        if t:
+            words(t)
+            mm(3, P, "CWQ", 0, "BQ", 0)
+        for b in range(3):
+            mm(b, 272, "BQ", 128 * b, "MCQ", 0)
+        for b in range(4):
+            act(v("FP", P * b, P * b + P), ps(4 + b, P), 1.0 / 64)
+            if b < 3:
+                act(v("XH", 256 * b, 256 * b + 256), ps(b, 256), 0.5)
+        tt(v("WR"), ps(3, P), v("PADM"), A.max)
+        for h in range(2):
+            ts(v("H%d" % h), v("WR"), v("IP", h, h + 1), A.is_equal, float(P), A.mult)
+        for h in range(2):
+            scan(v("PA%d" % h, 0, P, 1, True), v("NEG"), v("H%d" % h, 0, P, 1, True), 0.0, A.add, A.max)
+        for h in range(2):
+            scan(v("NX%d" % h, 0, P, 1, True), v("NEG"), v("H%d" % h, 0, P, 1, True), v("PA%d" % h, 0, 1), A.add, A.max)
+            cp(v("NX%d" % h, P, P + 1), v("PA%d" % h, 0, 1))
+        for b in range(3):
+            tt(v("RIF", 8 * b, 8 * b + 8), ps(b, 8, 256), v("BASE", 8 * b, 8 * b + 8), A.add)
+        cp(v("RI"), v("RIF"))
+        for h in range(2):
+            ts(v("DT", 2 * h, 1536, 4), v("NX%d" % h, 1, P + 1), M28, A.add, M28, A.subtract)
+        for h in range(2):
+            tt(v("DT", 2 * h + 1, 1536, 4), v("NX%d" % h, 1, P + 1), v("DT", 2 * h, 1536, 4), A.subtract)
+        qz("DQ", v("DT"))
+        for b in range(3):
+            mm(b, 256, "DQ", 128 * b, "TCQ", 0)
+            act(v("HI", 256 * b, 256 * b + 256), ps(b, 256))
+        for b in range(4):
+            act(v("FO", P * b, P * b + P), ps(4 + b, P), 1.0 / 64)
+        cpg(v("XG"), v("XH"), v("LW%d" % t, 0, 3))
+        tt(v("VV"), v("XG"), v("PADV"), A.add)
+        ts(v("ZZ"), v("XG"), 0.0, A.is_equal, 1024.0, A.mult)
+        ts(v("DI"), v("XG"), 2.0, A.mult)
+        tt(v("VV"), v("VV"), v("ZZ"), A.max)
+        for k in range(8):
+            ts(v("XK", 48 * k, 48 * k + 48), v("DI"), 1 << k, A.bitwise_and)
+        for k in range(8):
+            for b in range(3):
+                red(v("MN", b, b + 1), v("VV", 16 * b, 16 * b + 16), A.min)
+            for b in range(3):
+                if k < 7:
+                    ts(v("KL", 16 * b, 16 * b + 16), v("XK", 48 * k + 16 * b, 48 * k + 16 * b + 16), v("MN", b, b + 1), A.is_gt, 4096.0, A.mult)
+            ts(v("KEEP", k, 24, 8), v("MN"), float(1 << k), A.is_lt)
+            if k < 7:
+                tt(v("VV"), v("VV"), v("KL"), A.max)
+        tt(v("KB"), v("KEEP"), v("BJ"), A.mult)
+        ts(v("M0"), v("KB"), -1.0, A.mult, 1.0, A.add)
+        tt(v("KU"), v("KB"), v("KEEP"), A.subtract)
+        ts(v("M1"), v("KU"), 1.0, A.add)
+        ts(v("DROP"), v("KEEP"), -1.0, A.mult, 1.0, A.add)
+        for k in range(7):
+            n, s0 = 2 ** (7 - k), seg(k)
+            for b in range(3):
+                s = s0 + 2 * n * b
+                act(v("HH", n * b, n * b + n), v("HI", s + 1, s + 2 * n, 2), v("M1", 8 * b + k, 8 * b + k + 1))
+                ts(v("LO", n * b, n * b + n), v("HI", s, s + 2 * n, 2), v("M0", 8 * b + k, 8 * b + k + 1), A.mult)
+            tt(v("HI", seg(k + 1), seg(k + 1) + 3 * n), v("LO", 0, 3 * n), v("HH", 0, 3 * n), A.max)
+        cpg(v("RG"), v("HI"), v("RI"))
+        tt(v("RMX"), v("RG"), v("MASK"), A.mult)
+        tt(v("R1"), v("RMX", 0, 384, 2), v("RMX", 1, 384, 2), A.max)
+        tt(v("R2"), v("R1", 0, 192, 2), v("R1", 1, 192, 2), A.max)
+        tt(v("R3"), v("R2", 0, 96, 2), v("R2", 1, 96, 2), A.max)
+        tt(v("PR"), v("R3", 0, 48, 2), v("R3", 1, 48, 2), A.max)
+        tt(v("E1"), v("PR"), v("DROP"), A.mult)
+        tt(v("EN", 0, 24), v("E1"), v("KEEP"), A.subtract)
+        tr(v("T1"), v("EN"))
+        items = []
+        for k in range(8):
+            gr = (3 * t + k) % 8
+            for b in range(3):
+                p0 = 32 * (gr // 2) + 8 * b
+                c0 = 16 * (gr % 2)
+                yo = v("Y3", c0, c0 + 16)
+                items.append(("s" if (3 * k + b) % 2 else "a", T[yo[0]][p0:p0 + 8, yo[1]:yo[2]], T.T1[8 * b + k::32, 0:32], [v("T1")], [yo]))
+        dmas(items)
+        ye = v("Y3", 0, 32)
+        ts(v("FD0"), ye, 0.0, A.is_ge)
+        tt(v("FD"), v("FD0"), v("RM"), A.mult)
+        scan(v("Y3", 32, 64), v("D0R"), v("FD"), 0.0, A.mult, A.add)
+        ts(v("Y3", 64, 80), v("Z16"), v("Y3", 47, 48), A.add)
+        ts(v("Y3", 80, 96), v("Z16"), v("Y3", 63, 64), A.add)
+        tr(v("L3"), v("Y3"))
+        e, c1, tot = v("L3", 0, 24), v("L3", 32, 56), v("L3", 64, 88)
+        ts(v("LA"), e, 0.0, A.is_gt, 385.0, A.mult)
+        ts(v("LB"), e, 0.0, A.max)
+        tt(v("LC"), v("LA"), v("NC"), A.add)
+        tt(v("LD"), v("LC"), v("LB"), A.subtract)
+        ts(v("LE"), v("LD"), float(P), A.is_ge, float(P), A.mult)
+        tt(v("AA"), v("LD"), v("LE"), A.subtract)
+        cp(v("AL"), v("AA"))
+        scan(v("LF"), v("ONE24"), tot, 0.0, A.mult, A.add)
+        tt(v("LG"), c1, tot, A.subtract)
+        ts(v("LH"), e, 0.0, A.is_ge)
+        tt(v("LI"), v("LG"), v("LF"), A.add)
+        tt(v("LK"), v("LI"), v("LH"), A.subtract)
+        tt(v("LL"), v("JC"), v("LK"), A.subtract)
+        ts(v("LM"), v("LL"), v("LF", 23, 24), A.add)
+        tt(v("LN"), v("LK"), v("LM"), A.subtract)
+        tt(v("LP"), v("LN"), v("LH"), A.mult)
+        tt(v("LR"), v("LP"), v("LM"), A.add)
+        ts(v("LR"), v("LR"), v("RC"), A.mult)
+        tt(v("LG"), v("LR"), v("PADC"), A.add)
+        cp(v("PL"), v("LG"))
+        scat(v("LWW"), v("PL"), v("NROW"))
+        tt(v("LMK"), v("LWW", 0, K), v("MASK", 0, K), A.mult)
+        for c in range(6):
+            red(v("L6", c, c + 1), v("LMK", 16 * c, 16 * c + 16), A.add)
+        cp(v("L6U"), v("L6"))
+        for b in range(4):
+            ttg(v("TZ", 480 * b + K, 480 * b + 480), v("FP", P * b, P * b + P), v("AL"), v("FO", P * b, P * b + P), A.add)
+        for b in range(4):
+            z = v("TZ", 480 * b + K, 480 * b + 480)
+            o = v("ET", b, 4 * K, 4)
+            if b % 2:
+                cpg(o, z, v("L6U"))
+            else:
+                act(o, z, off=v("L6U"))
+        qz("EQ", v("ET"))
+        lt, rt = "el%d" % t, "er%d" % t
+        total[lt] = total[rt] = 2 * neng
+        sync("g", [v("EQ"), v("EQS")], [])
+        g.remote_dma(T.LQ[:, 0:K].bitcast(dt.uint8), T.EQ[:, 0:K].bitcast(dt.uint8), T.sem[rt], T.sem[lt], pid, rid, mask)
+        g.remote_dma(T.LQS[:, 0:K], T.EQS[:, 0:K], T.sem[rt], T.sem[lt], pid, rid, mask)
+        note("g", [v("EQ"), v("EQS")], [], lt, 2 * neng)
+        for q in ("LQ", "LQS"):
+            recs.setdefault(q, []).append(("w", v(q, 0, K)[:4], rt, 2 * neng, {rt: 2 * neng}))
+        ts(v("LA"), v("LG"), float(K), A.is_lt)
+        tt(v("LB"), v("LG"), v("N96"), A.subtract)
+        tt(v("LC"), v("LA"), v("LB"), A.mult)
+        tt(v("LD"), v("LC"), v("N96"), A.add)
+        cp(v("SL"), v("LD"))
+        if t == R - 1:
+            ts(v("LE"), v("AA"), -7.5, A.add, 1.0 / 16, A.mult)
+            ts(v("LF"), v("LE"), M23, A.add, M23, A.subtract)
+            ts(v("LI"), v("LF"), -4.0, A.mult)
+            tt(v("AJ", 0, 24), v("AA"), v("LI"), A.add)
+            tr(v("AJT"), v("AJ"))
+            ts(v("RMX", 0, K), v("LWW", 0, K), -7.5, A.add, 1.0 / 16, A.mult)
+            ts(v("RMX", 96, 96 + K), v("RMX", 0, K), M23, A.add, M23, A.subtract)
+            ts(v("RMX", 192, 192 + K), v("RMX", 96, 96 + K), -4.0, A.mult)
+            tt(v("SC", 0, K), v("LWW", 0, K), v("RMX", 192, 192 + K), A.add)
+            o = v("AJT")[1]
+            dmas([("s", T.al[:, C:C + K], T.SC[0:128:16, 0:K], [v("SC", 0, K)], [])]
+                 + [("s", T.al[gr:gr + 1, 0:C], T["FS"][32 * (gr // 2):32 * (gr // 2) + 24, o + 16 * (gr % 2):o + 16 * (gr % 2) + 12], [v("AJT")], []) for gr in range(8)])
+        if t == 0:
+            qz("VQ", v("VT"))
+            ts(v("PLA"), v("IOD"), v("PM"), A.add)
+            ts(v("PLB"), v("PLA"), -5.5, A.add, 1.0 / 12, A.mult)
+            ts(v("PLB"), v("PLB"), M23, A.add, M23, A.subtract)
+            ts(v("PLB"), v("PLB"), 4.0, A.mult)
+            tt(v("PLA"), v("PLA"), v("PLB"), A.add)
+            cp(v("PLOUT"), v("PLA"))
+        for b in range(4):
+            mm(4 + b, 128, "WQ", 128 * b, "LQ", 0, True, False)
+            mm(4 + b, 128, "EBQ", 128 * b, "LQ", 0, False, True)
+        for b in range(4):
+            o = v("TZ", 480 * b, 480 * b + K)
+            if b % 2:
+                ts(o, ps(4 + b, K), 0.03125, A.mult)
+            else:
+                act(o, ps(4 + b, K), 0.03125)
+        for b in range(4):
+            o, i = v("XT", b, 1536, 4), v("TZ", 480 * b, 480 * b + 480)
+            if b % 2:
+                cpg(o, i, v("SL"))
+            else:
+                act(o, i, off=v("SL"))
+        qz("XQ", v("XT"))
+    pickc(v("QC"), v("XQ"), v("PLOUT"))
+    act(v("QCS"), v("XQS"), off=v("PLOUT"))
+    mm(0, C, "VQ", 0, "QC", 0)
+    dmas([("s", T.oc[:, :], T.QC[:, :].bitcast(dt.uint8), [v("QC")], [])])
+    act(v("YO", 0, 144), ps(0, 144))
+    dmas([("s" if k % 2 else "a", T.osc[4 * k:4 * k + 4, :], T.QCS[32 * k:32 * k + 4, :], [v("QCS")], []) for k in range(4)])
+    cp(v("YO", 144, 288), ps(0, 144, 144))
+    dmas([("s", T.y[:, :], T.YO[:, :], [v("YO")], [])])
+    for tok in sorted(total):
+        if total[tok]:
+            g.wait_ge(T.sem[tok], total[tok])

@@ -2,7 +2,6 @@ from concourse.bass import DstId, RemoteDMATransfer
 from concourse.mybir import dt, AluOpType, AxisListType, ActivationFunctionType
 
 N, C, R, NG = 8, 288, 3, 8
-NB = 24
 P = 384
 K = 96
 
@@ -13,46 +12,55 @@ def _b(name, cols, dtype, where="sbuf"):
     _S[name] = (where, [128, cols], dtype)
 
 
-for _n, _c in (("XN", 1152), ("XT", 1536), ("UT", 1024), ("VT", 512), ("FP", 1536), ("FO", 1536), ("TZ", 1920), ("ET", 512), ("BT", 1536), ("DT", 1536),
+for _n, _c in (("XN", 1152), ("XT", 1536), ("UT", 1024), ("VT", 512), ("FP", 3072), ("FO", 1536), ("TZ", 1920), ("ET", 512), ("BT", 1536), ("DT", 1536),
                ("EB", 2048), ("TC", 1024), ("CW", 512), ("MC", 1088), ("WR", 384), ("H0", 384), ("H1", 384), ("NEG", 384), ("ONB", 128), ("ID", 128)):
     _b(_n, _c, "bfloat16")
 for _n, _c in (("XNQ", 288), ("XQ", 384), ("QC", 288), ("UQ", 256), ("VQ", 128), ("EQ", 128), ("LQ", 128), ("BQ", 384), ("DQ", 384),
                ("EBQ", 512), ("TCQ", 256), ("CWQ", 128), ("MCQ", 272), ("WQ", 512)):
     _b(_n, _c, "float8_e4m3fn_x4")
     _b(_n + "S", _c, "uint8")
-for _n, _c in (("SEL8", 8), ("ONE8", 8), ("POW", 24), ("INV", 8), ("IM8", 8), ("T8", 8), ("T8B", 8), ("T8C", 8), ("WP", 1), ("IW", 1), ("IW2", 1), ("WI", 256),
-               ("FLA", 256), ("FLB", 256), ("FLC", 256), ("NBT", 256), ("IP", 2), ("GE", 1), ("PM", 1), ("PMC", 1), ("RC", 1), ("NRC", 1), ("PML", 1), ("QROW", 384),
-               ("MASK", 384), ("PADM", 384), ("NROW", 384), ("IOA", 24), ("IOB", 24), ("IOC", 24), ("NC", 24), ("N96", 24), ("JC", 24), ("PADC", 24),
-               ("PADV", 48), ("BASE", 24), ("O256", 3), ("D0R", 32), ("RM", 32), ("ONE24", 24), ("Z16", 16), ("IOD", 18), ("PLA", 18), ("PLB", 18),
-               ("BJ", 24), ("BW", 24), ("W3", 3), ("W3B", 3), ("XH", 768), ("PA0", 384), ("PA1", 384), ("NX0", 385), ("NX1", 385), ("RIF", 24),
-               ("XG", 48), ("ZZ", 48), ("VV", 48), ("KL", 48), ("MN", 3), ("KEEP", 24), ("KB", 24), ("KU", 24), ("M0", 24), ("M1", 24), ("DROP", 24),
-               ("HI", 1536), ("LO", 384), ("HH", 384), ("RG", 384), ("RMX", 384), ("R1", 192), ("R2", 96), ("R3", 48), ("PR", 24), ("E1", 24), ("EN", 32),
-               ("T1", 32), ("Y3", 96), ("FD0", 32), ("FD", 32), ("L3", 96), ("LA", 24), ("LB", 24), ("LC", 24), ("LD", 24), ("LE", 24), ("LF", 24), ("LG", 24),
-               ("LH", 24), ("LI", 24), ("LK", 24), ("LL", 24), ("LM", 24), ("LN", 24), ("LP", 24), ("LR", 24), ("AA", 24), ("LWW", 384), ("LMK", 96), ("L6", 6),
-               ("AJ", 32), ("AJT", 32), ("YO", 288), ("SC", 384)):
+for _n, _c in (("WI", 256), ("FLA", 256), ("FLB", 256), ("FLC", 256), ("NBT", 256), ("QROW", 384), ("MASK", 384), ("PADM", 384), ("NROW", 384), ("XH", 768),
+               ("PA0", 384), ("PA1", 384), ("NX0", 385), ("NX1", 385), ("HI", 1536), ("LO", 384), ("HH", 384), ("LO2", 192), ("HH2", 192), ("RG", 384), ("RMX", 384), ("RSC", 384),
+               ("D0G", 192), ("EN", 32), ("T1", 32), ("Y3", 96), ("L3", 96), ("LWW", 384), ("LMK", 96), ("LSC", 96), ("YO", 288), ("SC", 480)):
     _b(_n, _c, "float32")
 for _n, _c in (("DI", 48), ("XK", 384)):
     _b(_n, _c, "int32")
-for _n, _c in (("WOUT", 4), ("LW0", 4), ("LW1", 4), ("LW2", 4), ("RI", 24), ("AL", 24), ("PL", 24), ("SL", 24), ("L6U", 6), ("PLIN", 24), ("PLOUT", 18)):
+for _n, _c in (("WOUT", 6), ("LW0", 6), ("LW1", 6), ("LW2", 6), ("RI", 24), ("AL", 24), ("PL", 24), ("SL", 24), ("L6U", 6), ("PLIN", 24), ("PLOUT", 18)):
     _b(_n, _c, "uint16")
 _b("PS", 4096, "float32", "psum")
-_SMALL, _WID, _at = {}, {}, 0
-for _n in [n for n in _S if _S[n][2] == "float32" and _S[n][0] == "sbuf" and _S[n][1][1] <= 48 and n not in ("T1", "EN", "MASK")]:
-    _SMALL[_n] = _at
-    _WID[_n] = _S[_n][1][1]
-    _at += -(-_S[_n][1][1] // 16) * 16
-    del _S[_n]
-_OWN = ("SEL8", "ONE8", "POW", "INV", "IM8", "T8", "T8B", "T8C", "WP", "IW", "IW2", "IP")
-_b("FS", _at, "float32")
-_b("FC", _at, "float32")
+_SMALL, _WID, _at = {}, {}, {"FC": 0, "FS": 0}
+
+
+def _small(buf, names, w):
+    for n in names.split():
+        _SMALL[n] = (buf, _at[buf])
+        _WID[n] = w
+        _at[buf] += -(-w // 16) * 16
+
+
+_small("FC", "SEL8 ONE8 INV IM8 T8 T8B T8C", 8)
+_small("FC", "POW", 24)
+_small("FC", "WP IW IW2 IP0 IP1", 1)
+_small("FS", "GE PM PMC RC NRC NRK PML", 1)
+_small("FS", "IOA IOB IOC NC N96 N385 JC PADC BASE ONE24 BJ BQO BW RIF KEEP KB KU M0 M1 DROP KQ E1", 24)
+_small("FS", "EZ EU0 EU TS CD BK BD JD UU A1 A2 MNN PO SA SB SD SE AJA AJB AJC AJD PLA PLB IOD", 24)
+_small("FS", "PADV PADW RST XG ZZ VV VS KL VT2 KL2", 48)
+_small("FS", "D0R RM FD0 FD CI CX AJ AJT", 32)
+_small("FS", "Z16", 16)
+_small("FS", "W3", 3)
+for _n in _at:
+    _b(_n, _at[_n], "float32")
+_b("D0L", 96, "float32")
 SCRATCH = _S
 SEMAPHORES = (["qv", "qa", "qp", "qg"] + ["d%d" % i for i in range(24)]
               + [n % t for t in range(R) for n in ("wr%d", "wl%d", "er%d", "el%d")])
-_BANKED = {"PS": 512}
 A = AluOpType
 ACT = ActivationFunctionType
 M23 = 1.5 * 2.0 ** 23
 M28 = 1.5 * 2.0 ** 28
+CY = 0.00083
+WAKE = 0.15
+DELTA = 0.05
 
 
 def rank_program(g, core, T, topo):
@@ -67,15 +75,17 @@ def rank_program(g, core, T, topo):
     TOK = {"v": "qv", "a": "qa", "p": "qp", "g": "qg"}
     total = {k: 0 for k in ("qv", "qa", "qp", "qg")}
     know = {e: {} for e in Q}
-    recs = {}
+    nodes = []
     nd = [0]
 
     def v(name, lo=0, hi=None, st=1, rev=False):
         if name in _SMALL:
-            buf, o = ("FC" if name in _OWN else "FS"), _SMALL[name]
-            w = _WID[name]
-            return (buf, o + lo, o + (w if hi is None else hi), st, rev)
+            buf, o = _SMALL[name]
+            return (buf, o + lo, o + (_WID[name] if hi is None else hi), st, rev)
         return (name, lo, SCRATCH[name][1][1] if hi is None else hi, st, rev)
+
+    def ps(bank, n, lo=0, st=1):
+        return v("PS", 512 * bank + lo, 512 * bank + lo + n, st)
 
     def ap(w):
         t = T[w[0]]
@@ -83,9 +93,15 @@ def rank_program(g, core, T, topo):
             return t[:, w[2] - 1:(w[1] - 1 if w[1] > 0 else None):-1]
         return t[:, w[1]:w[2]] if w[3] == 1 else t[:, w[1]:w[2]:w[3]]
 
+    def wid(w):
+        return len(range(w[1], w[2], w[3]))
+
+    def half(*ws):
+        return 0.5 if all(SCRATCH[w[0]][2] in ("bfloat16", "uint16") for w in ws) else 1.0
+
     def acc(w):
-        if w[0] in _BANKED:
-            return ("%s.%d" % (w[0], w[1] // 512), 0, 1, 1)
+        if w[0] == "PS":
+            return ("PS.%d" % (w[1] // 512), 0, 1, 1)
         return w[:4]
 
     def meet(a, b):
@@ -93,131 +109,110 @@ def rank_program(g, core, T, topo):
             return False
         return not (a[3] == b[3] and a[3] > 1 and (a[1] - b[1]) % a[3])
 
-    def sync(e, reads, writes):
-        need = {}
-        me = TOK.get(e)
-        for kind, accs in (("r", reads), ("w", writes)):
-            for x in accs:
-                for (k2, x2, tok, cnt, snap) in recs.get(x[0], ()):
-                    psum = x[0][:3] == "PS."
-                    if kind == "r" and k2 == "r" and not (psum and tok != me):
-                        continue
-                    if tok == me and (psum and me == "qp" or k2 == "r"):
-                        continue
-                    if not meet(x, x2) or know[e].get(tok, 0) >= cnt:
-                        continue
-                    if tok not in need or need[tok][0] < cnt:
-                        need[tok] = (cnt, snap)
-        for tok in sorted(need, key=lambda q: q == me):
-            cnt, snap = need[tok]
-            if know[e].get(tok, 0) >= cnt:
-                continue
-            if any(t2 != tok and s2[1].get(tok, 0) >= cnt for t2, s2 in need.items() if know[e].get(t2, 0) < s2[0]):
-                continue
-            Q[e].wait_ge(T.sem[tok], cnt)
-            for t3, c3 in list(snap.items()) + [(tok, cnt)]:
-                if know[e].get(t3, 0) < c3:
-                    know[e][t3] = c3
+    def covers(x, y):
+        return x[1] <= y[1] and x[2] >= y[2] and (x[3] == 1 or (x[3] == y[3] and (x[1] - y[1]) % x[3] == 0))
 
-    def note(e, reads, writes, tok, cnt):
-        snap = dict(know[e])
-        snap[tok] = cnt
-        for kind, accs in (("r", reads), ("w", writes)):
-            for x in accs:
-                l = recs.setdefault(x[0], [])
-                if kind == "w":
-                    l[:] = [o for o in l if not (x[1] <= o[1][1] and x[2] >= o[1][2] and (x[3] == 1 or (x[3] == o[1][3] and (x[1] - o[1][1]) % x[3] == 0)))]
-                else:
-                    l[:] = [o for o in l if not (o[0] == "r" and o[2] == tok and o[1] == x)]
-                l.append((kind, x, tok, cnt, snap))
-
-    def issue(e, fn, reads, writes):
-        reads, writes = [acc(x) for x in reads], [acc(x) for x in writes]
-        sync(e, reads, writes)
-        tok = TOK[e]
-        total[tok] += 1
-        fn().then_inc(T.sem[tok], 1)
-        note(e, reads, writes, tok, total[tok])
+    def node(e, fn, reads, writes, dur, lat=0.0, tok=None, cnt=0, kind="c"):
+        nodes.append({"e": e, "fn": fn, "r": [acc(x) for x in reads], "w": [acc(x) for x in writes], "dur": dur, "lat": lat, "tok": tok, "cnt": cnt, "kind": kind})
+        return len(nodes) - 1
 
     def dmas(items):
         tok = "d%d" % nd[0]
         nd[0] += 1
         total[tok] = 16 * len(items)
         for (e, o, i, rd, wr) in items:
-            sync(e, [acc(x) for x in rd], [acc(x) for x in wr if x is not None])
-        for (e, o, i, rd, wr) in items:
-            Q[e].dma_start(o, i).then_inc(T.sem[tok], 16)
-        for (e, o, i, rd, wr) in items:
-            note(e, [acc(x) for x in rd], [acc(x) for x in wr], tok, total[tok])
+            node(e, (lambda e=e, o=o, i=i: Q[e].dma_start(o, i)), rd, wr, 0.07, 2.0, tok, total[tok], "d")
 
     def isv(x):
         return x is not None and not isinstance(x, (int, float))
 
+    def cyc(n):
+        return max(64, n) * CY
+
     def ts(o, i, s1, op0, s2=None, op1=None):
         a1, a2 = (ap(s1) if isv(s1) else s1), (ap(s2) if isv(s2) else s2)
         rd = [i] + [x for x in (s1, s2) if isv(x)]
+        d = cyc(wid(o) * half(o, i))
         if op1 is None:
-            issue("v", lambda: g.vector.tensor_scalar(ap(o), ap(i), a1, None, op0), rd, [o])
+            node("v", lambda: g.vector.tensor_scalar(ap(o), ap(i), a1, None, op0), rd, [o], d)
         else:
-            issue("v", lambda: g.vector.tensor_scalar(ap(o), ap(i), a1, a2, op0, op1), rd, [o])
+            node("v", lambda: g.vector.tensor_scalar(ap(o), ap(i), a1, a2, op0, op1), rd, [o], d)
 
     def tt(o, a, b, op):
-        issue("v", lambda: g.vector.tensor_tensor(ap(o), ap(a), ap(b), op), [a, b], [o])
+        node("v", lambda: g.vector.tensor_tensor(ap(o), ap(a), ap(b), op), [a, b], [o], cyc(wid(o) * (1 if "PS" in (a[0], b[0]) else 2)))
+
+    def gath(off):
+        return 0.05 + 16 * wid(off) * 1.56 * CY
 
     def ttg(o, a, off, b, op):
-        issue("v", lambda: g.vector.tensor_tensor(ap(o), ap(a).indirect(ap(off)), ap(b), op), [a, off, b], [o])
+        node("v", lambda: g.vector.tensor_tensor(ap(o), ap(a).indirect(ap(off)), ap(b), op), [a, off, b], [o], gath(off))
 
     def cp(o, i):
-        issue("v", lambda: g.vector.tensor_copy(ap(o), ap(i)), [i], [o])
+        node("v", lambda: g.vector.tensor_copy(ap(o), ap(i)), [i], [o], cyc(wid(o) * half(o, i)))
 
     def cpg(o, i, off):
-        issue("v", lambda: g.vector.tensor_copy(ap(o), ap(i).indirect(ap(off))), [i, off], [o])
+        node("v", lambda: g.vector.tensor_copy(ap(o), ap(i).indirect(ap(off))), [i, off], [o], gath(off))
 
     def scat(o, off, i):
-        issue("v", lambda: g.vector.tensor_copy(ap(o).indirect(ap(off)), ap(i)), [i, off], [o])
+        node("v", lambda: g.vector.tensor_copy(ap(o).indirect(ap(off)), ap(i)), [i, off], [o], 0.05 + 3 * wid(i) * CY)
 
     def pickc(o, i, off):
-        issue("v", lambda: g.vector.tensor_copy(ap(o).bitcast(dt.uint32), ap(i).bitcast(dt.uint32).indirect(ap(off))), [i, off], [o])
+        node("v", lambda: g.vector.tensor_copy(ap(o).bitcast(dt.uint32), ap(i).bitcast(dt.uint32).indirect(ap(off))), [i, off], [o], gath(off))
 
     def red(o, i, op):
-        issue("v", lambda: g.vector.tensor_reduce(ap(o), ap(i), AxisListType.X, op), [i], [o])
+        node("v", lambda: g.vector.tensor_reduce(ap(o), ap(i), AxisListType.X, op), [i], [o], cyc(wid(i)))
 
     def scan(o, a, b, init, op0, op1):
         ini = ap(init) if isv(init) else init
-        issue("v", lambda: g.vector.tensor_tensor_scan(ap(o), ap(a), ap(b), ini, op0, op1), [a, b] + ([init] if isv(init) else []), [o])
+        node("v", lambda: g.vector.tensor_tensor_scan(ap(o), ap(a), ap(b), ini, op0, op1), [a, b] + ([init] if isv(init) else []), [o], cyc(wid(b)))
 
     def tr(o, i):
-        issue("v", lambda: g.vector.transpose(ap(o), ap(i)), [i], [o])
+        node("v", lambda: g.vector.transpose(ap(o), ap(i)), [i], [o], cyc(wid(i)))
 
     def ms(o, c):
-        issue("v", lambda: g.vector.memset(ap(o), c), [], [o])
+        node("v", lambda: g.vector.memset(ap(o), c), [], [o], cyc(wid(o) * half(o)))
 
     def qz(q, i, lo=0, hi=None):
         qv, sv = v(q, lo, hi), v(q + "S", lo, hi)
-        issue("v", lambda: g.vector.quantize_mx(ap(qv), ap(sv), ap(i)), [i], [qv, sv])
+        node("v", lambda: g.vector.quantize_mx(ap(qv), ap(sv), ap(i)), [i], [qv, sv], 0.012 + 0.00022 * wid(i))
 
     def act(o, i, scale=1.0, off=None):
         sc = ap(scale) if isv(scale) else scale
         rd = [i] + ([scale] if isv(scale) else []) + ([off] if off is not None else [])
         src = (lambda: ap(i).indirect(ap(off))) if off is not None else (lambda: ap(i))
+        d = 0.015 + gath(off) if off is not None else cyc(wid(i))
         if isv(scale) or scale != 1.0:
-            issue("a", lambda: g.scalar.activation(ap(o), src(), ACT.Copy, scale=sc), rd, [o])
+            node("a", lambda: g.scalar.activation(ap(o), src(), ACT.Copy, scale=sc), rd, [o], d)
         else:
-            issue("a", lambda: g.scalar.activation(ap(o), src(), ACT.Copy), rd, [o])
+            node("a", lambda: g.scalar.activation(ap(o), src(), ACT.Copy), rd, [o], d)
+
+    def actl(o, i, scale, bias):
+        node("a", lambda: g.scalar.activation(ap(o), ap(i), ACT.Identity, bias=bias, scale=scale), [i], [o], cyc(wid(i)))
 
     def mm(bank, n, l, ll, r, rl, start=True, stop=True):
         o = v("PS", 512 * bank, 512 * bank + n)
         lq, ls, rq, rs = v(l, ll, ll + 128), v(l + "S", ll, ll + 128), v(r, rl, rl + n), v(r + "S", rl, rl + n)
-        issue("p", lambda: g.tensor.matmul_mx(ap(o), ap(lq), ap(ls), ap(rq), ap(rs), start, stop), [lq, ls, rq, rs], [o])
+        node("p", lambda: g.tensor.matmul_mx(ap(o), ap(lq), ap(ls), ap(rq), ap(rs), start, stop), [lq, ls, rq, rs], [o], (n + 16) * CY * 1.2)
 
     def iota(o, pat, base=0, ch=0):
-        issue("g", lambda: g.iota(ap(o), pat, base, ch, allow_small_or_imprecise_dtypes=True), [], [o])
+        node("g", lambda: g.iota(ap(o), pat, base, ch, allow_small_or_imprecise_dtypes=True), [], [o], 0.13 + 2 * wid(o) * CY)
 
     def asel(o, i, pat, op, fill, base, ch):
-        issue("g", lambda: g.affine_select(ap(o), ap(i), pat, op, fill, base, ch), [i], [o])
+        node("g", lambda: g.affine_select(ap(o), ap(i), pat, op, fill, base, ch), [i], [o], 0.17 + 2 * wid(i) * CY)
 
-    def ps(bank, n, lo=0, st=1):
-        return v("PS", 512 * bank + lo, 512 * bank + lo + n, st)
+    def send(kind, t, parts, rd, calls, lands):
+        lt, rt = kind + "l%d" % t, kind + "r%d" % t
+        n = neng * calls
+        total[lt] = total[rt] = n
+
+        def fn():
+            for (o, i) in parts:
+                g.remote_dma(o, i, T.sem[rt], T.sem[lt], pid, rid, mask)
+        node("g", fn, rd, [], 0.3 * calls, 1.5, lt, n, "r")
+        nodes.append({"e": None, "fn": None, "r": [], "w": [acc(x) for x in lands], "dur": 2.4 + 0.6 * (calls - 1), "lat": 0.0, "tok": rt, "cnt": n, "kind": "x", "after": len(nodes) - 1})
+
+    def q24(k):
+        return 12 * (k // 4) + k % 4
 
     dmas([("s", T.XN[:, 0:1152], T.x[:, :], [], [v("XN")])])
     dmas([("a", T.UT[:, 0:512], T.u[:, :], [], [v("UT", 0, 512)]), ("a", T.UT[:, 512:1024], T.u[:, :], [], [v("UT", 512, 1024)])])
@@ -226,70 +221,38 @@ def rank_program(g, core, T, topo):
 
     ms(v("ONE8"), 1.0)
     ms(v("ONB"), 1.0)
-    iota(v("IP", 0, 1), [[0, 1]], 0, 1)
+    iota(v("IP0"), [[0, 1]], 0, 1)
     asel(v("T8"), v("ONE8"), [[-16, 8]], A.is_ge, 0.0, 0, 1)
     iota(v("IOA"), [[12, 24]])
-    iota(v("IP", 1, 2), [[0, 1]], 128, 1)
     asel(v("SEL8"), v("ONE8"), [[-16, 8]], A.is_equal, 0.0, 0, 1)
     iota(v("WI"), [[1, 256]])
     asel(v("ID"), v("ONB"), [[-1, 128]], A.is_equal, 0.0, 0, 1)
     iota(v("QROW"), [[0, 24], [1, 16]])
+    iota(v("IP1"), [[0, 1]], 128, 1)
     red(v("GE"), v("T8"), A.add)
     ts(v("PMC"), v("GE"), -16.0, A.mult, 16.0, A.add)
-    tt(v("PM"), v("PMC"), v("IP", 0, 1), A.add)
+    tt(v("PM"), v("PMC"), v("IP0"), A.add)
     ts(v("PML"), v("PM"), 11.0, A.min)
     ts(v("PLIN"), v("IOA"), v("PML"), A.add)
     qz("UQ", v("UT"))
     qz("XNQ", v("XN"))
     pickc(v("XQ"), v("XNQ"), v("PLIN"))
     act(v("XQS"), v("XNQS"), off=v("PLIN"))
-    ms(v("BT"), 0.0)
+    for e in (2, 3):
+        ms(v("BT", e, 1536, 4), 0.0)
     for i in range(8):
         ms(v("POW", i, 24, 8), 2.0 ** i)
-    iota(v("O256"), [[256, 3]])
-
-    def words(t):
-        u0 = (3 * t % 8) * 16
-        for b in range(3):
-            mm(b, 128, "XQ", 128 * b, "UQ", u0)
-        mm(3, P, "UQ", u0, "XQ", 0)
-        if t:
-            for b in range(4):
-                mm(4 + b, P, "EBQ", 128 * b, "XQ", 0)
-        for b in range(3):
-            ts(v("BJ", 8 * b, 8 * b + 8), ps(b, 128, 0, 16), 0.0, A.is_gt)
-        tt(v("BW"), v("BJ"), v("POW"), A.mult)
-        for b in range(3):
-            red(v("W3", b, b + 1), v("BW", 8 * b, 8 * b + 8), A.add)
-        tt(v("W3B"), v("W3"), v("O256"), A.add)
-        cp(v("WOUT", 0, 3), v("W3B"))
-        lt, rt = "wl%d" % t, "wr%d" % t
-        total[lt] = total[rt] = neng
-        src = v("WOUT", 0, 3)
-        rd = [src]
-        if t == 0:
-            rd = rd + [v("LQ"), v("LQS")]
-        sync("g", rd, [])
-        g.remote_dma(T["LW%d" % t][:, 0:3], T.WOUT[:, 0:3], T.sem[rt], T.sem[lt], pid, rid, mask)
-        note("g", [src], [], lt, neng)
-        recs.setdefault("LW%d" % t, []).append(("w", v("LW%d" % t)[:4], rt, neng, {rt: neng}))
-        ts(v("BT", 0, 1536, 4), ps(3, P), 0.0, A.is_gt)
-        ts(v("BT", 1, 1536, 4), ps(3, P), 0.0, A.is_le)
-        qz("BQ", v("BT"))
-
+    ms(v("WOUT"), 0.0)
     ms(v("ET"), 0.0)
     qz("LQ", v("ET"))
-    words(0)
-    red_in = v("T8B")
-    issue("v", lambda: g.vector.reciprocal(ap(v("INV")), ap(v("POW", 0, 8))), [v("POW", 0, 8)], [v("INV")])
-    tt(red_in, v("SEL8"), v("POW", 0, 8), A.mult)
-    red(v("WP"), red_in, A.add)
+    node("v", lambda: g.vector.reciprocal(ap(v("INV")), ap(v("POW", 0, 8))), [v("POW", 0, 8)], [v("INV")], 0.25)
+    tt(v("T8B"), v("SEL8"), v("POW", 0, 8), A.mult)
+    red(v("WP"), v("T8B"), A.add)
     tt(v("T8C"), v("SEL8"), v("INV"), A.mult)
     red(v("IW"), v("T8C"), A.add)
     ms(v("CW"), 0.0)
-    ts(v("CW", 0, 512, 4), v("ONB"), v("WP"), A.mult)
+    act(v("CW", 0, 512, 4), v("ONB"), v("WP"))
     qz("CWQ", v("CW"))
-    mm(3, P, "CWQ", 0, "BQ", 0)
     asel(v("IM8"), v("INV"), [[-16, 8]], A.is_gt, 0.0, 0, 1)
     ms(v("MC"), 0.0)
     ts(v("IW2"), v("IW"), 0.5, A.mult)
@@ -299,46 +262,48 @@ def rank_program(g, core, T, topo):
     ts(v("FLC"), v("FLB"), M23, A.add, M23, A.subtract)
     ts(v("FLC"), v("FLC"), -2.0, A.mult)
     tt(v("FLB"), v("FLA"), v("FLC"), A.add)
-    ts(v("NBT"), v("FLB"), -1.0, A.mult, 1.0, A.add)
-    ts(v("MC", 0, 1024, 4), v("NBT"), v("WP"), A.mult)
-    ts(v("MC", 1, 1024, 4), v("FLB"), v("WP"), A.mult)
+    actl(v("NBT"), v("FLB"), -1.0, 1.0)
+    act(v("MC", 0, 1024, 4), v("NBT"), v("WP"))
+    act(v("MC", 1, 1024, 4), v("FLB"), v("WP"))
     ts(v("MC", 1024, 1056, 4), v("IM8"), v("WP"), A.mult)
     cp(v("MC", 1025, 1056, 4), v("SEL8"))
     qz("MCQ", v("MC"))
     ms(v("EB"), 0.0)
     for b in range(4):
-        ts(v("EB", 512 * b + b, 512 * b + 512, 4), v("ID"), 32.0, A.mult)
+        act(v("EB", 512 * b + b, 512 * b + 512, 4), v("ID"), 32.0)
     qz("EBQ", v("EB"))
-    for b in range(4):
-        mm(4 + b, P, "EBQ", 128 * b, "XQ", 0)
     ms(v("TC"), 0.0)
     for e in range(4):
-        cp(v("TC", 512 * (e // 2) + e, 512 * (e // 2) + 512, 4), v("ID"))
+        act(v("TC", 512 * (e // 2) + e, 512 * (e // 2) + 512, 4), v("ID"))
     qz("TCQ", v("TC"))
     ms(v("NEG"), -1.0)
-    ms(v("DT"), 0.0)
-    ms(v("HI"), 0.0)
+    ms(v("HI", 1520, 1536), 0.0)
     ms(v("EN"), 0.0)
     ms(v("Y3"), 0.0)
     ms(v("AJ"), 0.0)
     ms(v("Z16"), 0.0)
     ms(v("ONE24"), 1.0)
-    ms(v("D0R"), 1.0)
-    ms(v("D0R", 0, 32, 16), 0.0)
+    for n, w in (("D0R", 32), ("D0L", 96), ("D0G", 192)):
+        ms(v(n), 1.0)
+        ms(v(n, 0, w, 16), 0.0)
+    ms(v("RST"), 0.0)
+    ms(v("RST", 0, 48, 16), 2048.0)
+    for k in range(8):
+        iota(v("BASE", q24(k), q24(k) + 9, 4), [[2 ** (8 - k), 3]], 3 * (512 - 2 ** (9 - k)) - (1440 if k > 3 else 0))
     iota(v("NROW"), [[1, P]])
     iota(v("IOB"), [[16, 24]])
     iota(v("IOC"), [[4, 24]], 276)
-    for k in range(8):
-        iota(v("BASE", k, 24, 8), [[2 ** (8 - k), 3]], 3 * (512 - 2 ** (9 - k)))
-    iota(v("IOD"), [[16, 18]])
-    ts(v("MASK"), v("QROW"), v("PM"), A.is_equal)
+    iota(v("IOD", 0, 18), [[16, 18]])
     ts(v("PADM"), v("QROW"), 12.0, A.is_ge, 1000.0, A.mult)
-    ts(v("PADV"), v("QROW", 0, 48), 12.0, A.is_ge, 1024.0, A.mult)
-    ts(v("RM"), v("QROW", 0, 32), 12.0, A.is_lt)
-    ts(v("RC"), v("PM"), 12.0, A.is_lt)
     ts(v("NRC"), v("PM"), 12.0, A.is_ge)
+    ts(v("NRK"), v("NRC"), 1024.0, A.mult)
+    ts(v("PADW"), v("QROW", 0, 48), 12.0, A.is_ge, 1024.0, A.mult)
+    ts(v("PADV"), v("PADW"), v("NRK"), A.add)
+    ts(v("MASK"), v("QROW"), v("PM"), A.is_equal)
+    ts(v("RM"), v("QROW", 0, 32), 12.0, A.is_lt)
     ts(v("NC"), v("IOB"), v("PM"), A.add)
     ts(v("N96"), v("NC"), 96.0, A.add)
+    ts(v("N385"), v("NC"), 385.0, A.add)
     ts(v("JC"), v("IOA"), v("PM"), A.add)
     ts(v("PADC"), v("IOC"), v("PM"), A.add, v("NRC"), A.mult)
 
@@ -346,159 +311,172 @@ def rank_program(g, core, T, topo):
         return 3 * (512 - 2 ** (9 - k))
 
     for t in range(R):
-        if t:
-            words(t)
-            mm(3, P, "CWQ", 0, "BQ", 0)
+        u0 = (3 * t % 8) * 16
+        for b in range(3):
+            mm(b, 128, "XQ", 128 * b, "UQ", u0)
+        mm(3, P, "UQ", u0, "XQ", 0)
+        for b in range(3):
+            ts(v("BJ", 8 * b, 8 * b + 8), ps(b, 128, 0, 16), 0.0, A.is_gt)
+        tt(v("BW"), v("BJ"), v("POW"), A.mult)
+        for b in range(3):
+            red(v("W3", b, b + 1), v("BW", 8 * b, 8 * b + 8), A.add)
+        for b in range(3):
+            ts(v("WOUT", 2 * b, 2 * b + 1), v("W3", b, b + 1), 0.0, A.add)
+        lw = "LW%d" % t
+        send("w", t, [(T[lw][:, 0:6], T.WOUT[:, 0:6])], [v("WOUT")] + ([v("LQ"), v("LQS")] if t == 0 else []), 1, [v(lw)])
+        for b in range(3):
+            for h in range(2):
+                cp(v("BQO", 12 * h + 4 * b, 12 * h + 4 * b + 4), v("BJ", 8 * b + 4 * h, 8 * b + 4 * h + 4))
+        ts(v("BT", 0, 1536, 4), ps(3, P), 0.0, A.is_gt)
+        actl(v("BT", 1, 1536, 4), v("BT", 0, 1536, 4), -1.0, 1.0)
+        qz("BQ", v("BT"))
+        mm(3, P, "CWQ", 0, "BQ", 0)
         for b in range(3):
             mm(b, 272, "BQ", 128 * b, "MCQ", 0)
-        for b in range(4):
-            act(v("FP", P * b, P * b + P), ps(4 + b, P), 1.0 / 64)
-            if b < 3:
-                act(v("XH", 256 * b, 256 * b + 256), ps(b, 256), 0.5)
+            act(v("XH", 256 * b, 256 * b + 256), ps(b, 256), 0.5)
+            for h in range(2):
+                q = 12 * h + 4 * b
+                tt(v("RIF", q, q + 4), ps(b, 4, 256 + 4 * h), v("BASE", q, q + 4), A.add)
+        cp(v("RI"), v("RIF"))
         tt(v("WR"), ps(3, P), v("PADM"), A.max)
         for h in range(2):
-            ts(v("H%d" % h), v("WR"), v("IP", h, h + 1), A.is_equal, float(P), A.mult)
-        for h in range(2):
+            ts(v("H%d" % h), v("WR"), v("IP%d" % h), A.is_equal, float(P), A.mult)
             scan(v("PA%d" % h, 0, P, 1, True), v("NEG"), v("H%d" % h, 0, P, 1, True), 0.0, A.add, A.max)
-        for h in range(2):
             scan(v("NX%d" % h, 0, P, 1, True), v("NEG"), v("H%d" % h, 0, P, 1, True), v("PA%d" % h, 0, 1), A.add, A.max)
             cp(v("NX%d" % h, P, P + 1), v("PA%d" % h, 0, 1))
-        for b in range(3):
-            tt(v("RIF", 8 * b, 8 * b + 8), ps(b, 8, 256), v("BASE", 8 * b, 8 * b + 8), A.add)
-        cp(v("RI"), v("RIF"))
-        for h in range(2):
             ts(v("DT", 2 * h, 1536, 4), v("NX%d" % h, 1, P + 1), M28, A.add, M28, A.subtract)
-        for h in range(2):
             tt(v("DT", 2 * h + 1, 1536, 4), v("NX%d" % h, 1, P + 1), v("DT", 2 * h, 1536, 4), A.subtract)
         qz("DQ", v("DT"))
         for b in range(3):
             mm(b, 256, "DQ", 128 * b, "TCQ", 0)
             act(v("HI", 256 * b, 256 * b + 256), ps(b, 256))
         for b in range(4):
+            mm(4 + b, P, "EBQ", 128 * b, "XQ", 0)
+            act(v("FP", 768 * b, 768 * b + P), ps(4 + b, P), 1.0 / 64)
+            act(v("FP", 768 * b + P, 768 * b + 768), ps(4 + b, P), 1.0 / 64)
             act(v("FO", P * b, P * b + P), ps(4 + b, P), 1.0 / 64)
-        cpg(v("XG"), v("XH"), v("LW%d" % t, 0, 3))
-        tt(v("VV"), v("XG"), v("PADV"), A.add)
+        for b in range(3):
+            cpg(v("XG", 16 * b, 16 * b + 16), v("XH", 256 * b, 256 * b + 256), v(lw, 2 * b, 2 * b + 1))
         ts(v("ZZ"), v("XG"), 0.0, A.is_equal, 1024.0, A.mult)
-        ts(v("DI"), v("XG"), 2.0, A.mult)
+        tt(v("VV"), v("XG"), v("PADV"), A.add)
         tt(v("VV"), v("VV"), v("ZZ"), A.max)
+        ts(v("DI"), v("XG"), 2.0, A.mult)
         for k in range(8):
-            ts(v("XK", 48 * k, 48 * k + 48), v("DI"), 1 << k, A.bitwise_and)
+            if k < 7:
+                ts(v("XK", 48 * k, 48 * k + 48), v("DI"), 1 << k, A.bitwise_and)
         for k in range(8):
-            for b in range(3):
-                red(v("MN", b, b + 1), v("VV", 16 * b, 16 * b + 16), A.min)
+            vs, kl = ("VS", "KL") if k % 2 else ("VT2", "KL2")
+            scan(v(vs), v("RST"), v("VV"), 4096.0, A.add, A.min)
             for b in range(3):
                 if k < 7:
-                    ts(v("KL", 16 * b, 16 * b + 16), v("XK", 48 * k + 16 * b, 48 * k + 16 * b + 16), v("MN", b, b + 1), A.is_gt, 4096.0, A.mult)
-            ts(v("KEEP", k, 24, 8), v("MN"), float(1 << k), A.is_lt)
+                    ts(v(kl, 16 * b, 16 * b + 16), v("XK", 48 * k + 16 * b, 48 * k + 16 * b + 16), v(vs, 16 * b + 15, 16 * b + 16), A.is_gt, 4096.0, A.mult)
+            ts(v("KEEP", q24(k), q24(k) + 9, 4), v(vs, 15, 48, 16), float(1 << k), A.is_lt)
             if k < 7:
-                tt(v("VV"), v("VV"), v("KL"), A.max)
-        tt(v("KB"), v("KEEP"), v("BJ"), A.mult)
-        ts(v("M0"), v("KB"), -1.0, A.mult, 1.0, A.add)
-        tt(v("KU"), v("KB"), v("KEEP"), A.subtract)
-        ts(v("M1"), v("KU"), 1.0, A.add)
-        ts(v("DROP"), v("KEEP"), -1.0, A.mult, 1.0, A.add)
-        for k in range(7):
-            n, s0 = 2 ** (7 - k), seg(k)
-            for b in range(3):
-                s = s0 + 2 * n * b
-                act(v("HH", n * b, n * b + n), v("HI", s + 1, s + 2 * n, 2), v("M1", 8 * b + k, 8 * b + k + 1))
-                ts(v("LO", n * b, n * b + n), v("HI", s, s + 2 * n, 2), v("M0", 8 * b + k, 8 * b + k + 1), A.mult)
-            tt(v("HI", seg(k + 1), seg(k + 1) + 3 * n), v("LO", 0, 3 * n), v("HH", 0, 3 * n), A.max)
-        cpg(v("RG"), v("HI"), v("RI"))
-        tt(v("RMX"), v("RG"), v("MASK"), A.mult)
-        tt(v("R1"), v("RMX", 0, 384, 2), v("RMX", 1, 384, 2), A.max)
-        tt(v("R2"), v("R1", 0, 192, 2), v("R1", 1, 192, 2), A.max)
-        tt(v("R3"), v("R2", 0, 96, 2), v("R2", 1, 96, 2), A.max)
-        tt(v("PR"), v("R3", 0, 48, 2), v("R3", 1, 48, 2), A.max)
-        tt(v("E1"), v("PR"), v("DROP"), A.mult)
-        tt(v("EN", 0, 24), v("E1"), v("KEEP"), A.subtract)
+                tt(v("VV"), v("VV"), v(kl), A.max)
+            if k % 4 == 3:
+                lo, hi = 3 * k - 9, 3 * k + 3
+                tt(v("KB", lo, hi), v("KEEP", lo, hi), v("BQO", lo, hi), A.mult)
+                ts(v("M0", lo, hi), v("KB", lo, hi), -1.0, A.mult, 1.0, A.add)
+                tt(v("KU", lo, hi), v("KB", lo, hi), v("KEEP", lo, hi), A.subtract)
+                ts(v("M1", lo, hi), v("KU", lo, hi), 1.0, A.add)
+                ts(v("DROP", lo, hi), v("KEEP", lo, hi), -1.0, A.mult, 1.0, A.add)
+                ts(v("KQ", lo, hi), v("KEEP", lo, hi), 0.25, A.mult)
+        for k in range(8):
+            if k < 7:
+                n, s0 = 2 ** (7 - k), seg(k)
+                lo, hh = ("LO2", "HH2") if k % 2 else ("LO", "HH")
+                for b in range(3):
+                    s, m = s0 + 2 * n * b, q24(k) + 4 * b
+                    act(v(hh, n * b, n * b + n), v("HI", s + 1, s + 2 * n, 2), v("M1", m, m + 1))
+                    ts(v(lo, n * b, n * b + n), v("HI", s, s + 2 * n, 2), v("M0", m, m + 1), A.mult)
+                tt(v("HI", seg(k + 1), seg(k + 1) + 3 * n), v(lo, 0, 3 * n), v(hh, 0, 3 * n), A.max)
+            if k % 4 == 3:
+                h = k // 4
+                o = 192 * h
+                cpg(v("RG", o, o + 192), v("HI", 1440 * h, 1440 + 96 * h), v("RI", 12 * h, 12 * h + 12))
+                tt(v("RMX", o, o + 192), v("RG", o, o + 192), v("MASK", 0, 192), A.mult)
+                scan(v("RSC", o, o + 192), v("D0G"), v("RMX", o, o + 192), 0.0, A.mult, A.max)
+                tt(v("E1", 12 * h, 12 * h + 12), v("RSC", o + 15, o + 192, 16), v("DROP", 12 * h, 12 * h + 12), A.mult)
+                tt(v("EN", 12 * h, 12 * h + 12), v("E1", 12 * h, 12 * h + 12), v("KQ", 12 * h, 12 * h + 12), A.subtract)
         tr(v("T1"), v("EN"))
         items = []
         for k in range(8):
             gr = (3 * t + k) % 8
             for b in range(3):
-                p0 = 32 * (gr // 2) + 8 * b
-                c0 = 16 * (gr % 2)
-                yo = v("Y3", c0, c0 + 16)
-                items.append(("s" if (3 * k + b) % 2 else "a", T[yo[0]][p0:p0 + 8, yo[1]:yo[2]], T.T1[8 * b + k::32, 0:32], [v("T1")], [yo]))
+                p0, c0 = 32 * (gr // 2) + 8 * b, 16 * (gr % 2)
+                items.append(("s" if (3 * k + b) % 2 else "a", T.Y3[p0:p0 + 8, c0:c0 + 16], T.T1[q24(k) + 4 * b::32, 0:32], [v("T1")], [v("Y3", c0, c0 + 16)]))
         dmas(items)
-        ye = v("Y3", 0, 32)
-        ts(v("FD0"), ye, 0.0, A.is_ge)
+        tr(v("L3", 0, 32), v("Y3", 0, 32))
+        e = v("L3", 0, 24)
+        ts(v("EZ"), e, 0.0, A.is_le, 385.0, A.mult)
+        tt(v("EU0"), v("N385"), e, A.subtract)
+        tt(v("EU"), v("EU0"), v("EZ"), A.subtract)
+        cp(v("AL"), v("EU"))
+        ts(v("FD0"), v("Y3", 0, 32), 0.0, A.is_ge)
         tt(v("FD"), v("FD0"), v("RM"), A.mult)
-        scan(v("Y3", 32, 64), v("D0R"), v("FD"), 0.0, A.mult, A.add)
-        ts(v("Y3", 64, 80), v("Z16"), v("Y3", 47, 48), A.add)
-        ts(v("Y3", 80, 96), v("Z16"), v("Y3", 63, 64), A.add)
-        tr(v("L3"), v("Y3"))
-        e, c1, tot = v("L3", 0, 24), v("L3", 32, 56), v("L3", 64, 88)
-        ts(v("LA"), e, 0.0, A.is_gt, 385.0, A.mult)
-        ts(v("LB"), e, 0.0, A.max)
-        tt(v("LC"), v("LA"), v("NC"), A.add)
-        tt(v("LD"), v("LC"), v("LB"), A.subtract)
-        ts(v("LE"), v("LD"), float(P), A.is_ge, float(P), A.mult)
-        tt(v("AA"), v("LD"), v("LE"), A.subtract)
-        cp(v("AL"), v("AA"))
-        scan(v("LF"), v("ONE24"), tot, 0.0, A.mult, A.add)
-        tt(v("LG"), c1, tot, A.subtract)
-        ts(v("LH"), e, 0.0, A.is_ge)
-        tt(v("LI"), v("LG"), v("LF"), A.add)
-        tt(v("LK"), v("LI"), v("LH"), A.subtract)
-        tt(v("LL"), v("JC"), v("LK"), A.subtract)
-        ts(v("LM"), v("LL"), v("LF", 23, 24), A.add)
-        tt(v("LN"), v("LK"), v("LM"), A.subtract)
-        tt(v("LP"), v("LN"), v("LH"), A.mult)
-        tt(v("LR"), v("LP"), v("LM"), A.add)
-        ts(v("LR"), v("LR"), v("RC"), A.mult)
-        tt(v("LG"), v("LR"), v("PADC"), A.add)
-        cp(v("PL"), v("LG"))
+        scan(v("CI"), v("D0R"), v("FD"), 0.0, A.mult, A.add)
+        tt(v("CX"), v("CI"), v("FD"), A.subtract)
+        for h in range(2):
+            last = v("CI", 16 * h + 15, 16 * h + 16)
+            ts(v("Y3", 32 + 16 * h, 48 + 16 * h), v("CX", 16 * h, 16 * h + 16), last, A.subtract)
+            ts(v("Y3", 64 + 16 * h, 80 + 16 * h), v("Z16"), last, A.add)
+        tr(v("L3", 32, 96), v("Y3", 32, 96))
+        ts(v("BK"), e, 0.0, A.is_lt, 4096.0, A.mult)
+        ts(v("BD"), e, 0.0, A.is_ge, 4096.0, A.mult)
+        tt(v("JD"), v("JC"), v("BD"), A.add)
+        scan(v("TS"), v("ONE24"), v("L3", 64, 88), 0.0, A.mult, A.add)
+        tt(v("CD"), v("L3", 32, 56), v("TS"), A.add)
+        ts(v("UU"), v("JD"), v("TS", 23, 24), A.add)
+        tt(v("A1"), v("CD"), v("BK"), A.add)
+        tt(v("A2"), v("UU"), v("CD"), A.subtract)
+        tt(v("MNN"), v("A1"), v("A2"), A.min)
+        tt(v("PO"), v("MNN"), v("PADC"), A.max)
+        cp(v("PL"), v("PO"))
         scat(v("LWW"), v("PL"), v("NROW"))
         tt(v("LMK"), v("LWW", 0, K), v("MASK", 0, K), A.mult)
-        for c in range(6):
-            red(v("L6", c, c + 1), v("LMK", 16 * c, 16 * c + 16), A.add)
-        cp(v("L6U"), v("L6"))
+        scan(v("LSC"), v("D0L"), v("LMK"), 0.0, A.mult, A.add)
+        cp(v("L6U"), v("LSC", 15, K, 16))
         for b in range(4):
-            ttg(v("TZ", 480 * b + K, 480 * b + 480), v("FP", P * b, P * b + P), v("AL"), v("FO", P * b, P * b + P), A.add)
+            ttg(v("TZ", 480 * b + K, 480 * b + 480), v("FP", 768 * b, 768 * b + 768), v("AL"), v("FO", P * b, P * b + P), A.add)
         for b in range(4):
-            z = v("TZ", 480 * b + K, 480 * b + 480)
-            o = v("ET", b, 4 * K, 4)
+            z, o = v("TZ", 480 * b + K, 480 * b + 480), v("ET", b, 4 * K, 4)
             if b % 2:
                 cpg(o, z, v("L6U"))
             else:
                 act(o, z, off=v("L6U"))
         qz("EQ", v("ET"))
-        lt, rt = "el%d" % t, "er%d" % t
-        total[lt] = total[rt] = 2 * neng
-        sync("g", [v("EQ"), v("EQS")], [])
-        g.remote_dma(T.LQ[:, 0:K].bitcast(dt.uint8), T.EQ[:, 0:K].bitcast(dt.uint8), T.sem[rt], T.sem[lt], pid, rid, mask)
-        g.remote_dma(T.LQS[:, 0:K], T.EQS[:, 0:K], T.sem[rt], T.sem[lt], pid, rid, mask)
-        note("g", [v("EQ"), v("EQS")], [], lt, 2 * neng)
-        for q in ("LQ", "LQS"):
-            recs.setdefault(q, []).append(("w", v(q, 0, K)[:4], rt, 2 * neng, {rt: 2 * neng}))
-        ts(v("LA"), v("LG"), float(K), A.is_lt)
-        tt(v("LB"), v("LG"), v("N96"), A.subtract)
-        tt(v("LC"), v("LA"), v("LB"), A.mult)
-        tt(v("LD"), v("LC"), v("N96"), A.add)
-        cp(v("SL"), v("LD"))
+        send("e", t, [(T.LQ[:, 0:K].bitcast(dt.uint8), T.EQ[:, 0:K].bitcast(dt.uint8)), (T.LQS[:, 0:K], T.EQS[:, 0:K])],
+             [v("EQ"), v("EQS")], 2, [v("LQ", 0, K), v("LQS", 0, K)])
+        ts(v("SA"), v("PO"), float(K), A.is_lt)
+        tt(v("SB"), v("PO"), v("N96"), A.subtract)
+        tt(v("SD"), v("SA"), v("SB"), A.mult)
+        tt(v("SE"), v("SD"), v("N96"), A.add)
+        cp(v("SL"), v("SE"))
         if t == R - 1:
-            ts(v("LE"), v("AA"), -7.5, A.add, 1.0 / 16, A.mult)
-            ts(v("LF"), v("LE"), M23, A.add, M23, A.subtract)
-            ts(v("LI"), v("LF"), -4.0, A.mult)
-            tt(v("AJ", 0, 24), v("AA"), v("LI"), A.add)
+            ts(v("AJA"), v("EU"), float(P), A.is_ge, -float(P), A.mult)
+            tt(v("AJB"), v("EU"), v("AJA"), A.add)
+            ts(v("AJC"), v("AJB"), M23, A.add, M23, A.subtract)
+            ts(v("AJB"), v("AJC"), -7.5, A.add, 1.0 / 16, A.mult)
+            ts(v("AJD"), v("AJB"), M23, A.add, M23, A.subtract)
+            ts(v("AJA"), v("AJD"), -4.0, A.mult)
+            tt(v("AJ", 0, 24), v("AJC"), v("AJA"), A.add)
             tr(v("AJT"), v("AJ"))
-            ts(v("RMX", 0, K), v("LWW", 0, K), -7.5, A.add, 1.0 / 16, A.mult)
-            ts(v("RMX", 96, 96 + K), v("RMX", 0, K), M23, A.add, M23, A.subtract)
-            ts(v("RMX", 192, 192 + K), v("RMX", 96, 96 + K), -4.0, A.mult)
-            tt(v("SC", 0, K), v("LWW", 0, K), v("RMX", 192, 192 + K), A.add)
-            o = v("AJT")[1]
+            ts(v("SC", 96, 192), v("LWW", 0, K), -7.5, A.add, 1.0 / 16, A.mult)
+            ts(v("SC", 192, 288), v("SC", 96, 192), M23, A.add, M23, A.subtract)
+            ts(v("SC", 288, 384), v("SC", 192, 288), -4.0, A.mult)
+            tt(v("SC", 0, K), v("LWW", 0, K), v("SC", 288, 384), A.add)
+            o = v("AJT")
             dmas([("s", T.al[:, C:C + K], T.SC[0:128:16, 0:K], [v("SC", 0, K)], [])]
-                 + [("s", T.al[gr:gr + 1, 0:C], T["FS"][32 * (gr // 2):32 * (gr // 2) + 24, o + 16 * (gr % 2):o + 16 * (gr % 2) + 12], [v("AJT")], []) for gr in range(8)])
+                 + [("s", T.al[gr:gr + 1, 0:C], T[o[0]][32 * (gr // 2):32 * (gr // 2) + 24, o[1] + 16 * (gr % 2):o[1] + 16 * (gr % 2) + 12], [o], []) for gr in range(8)])
         if t == 0:
             qz("VQ", v("VT"))
-            ts(v("PLA"), v("IOD"), v("PM"), A.add)
-            ts(v("PLB"), v("PLA"), -5.5, A.add, 1.0 / 12, A.mult)
-            ts(v("PLB"), v("PLB"), M23, A.add, M23, A.subtract)
-            ts(v("PLB"), v("PLB"), 4.0, A.mult)
-            tt(v("PLA"), v("PLA"), v("PLB"), A.add)
-            cp(v("PLOUT"), v("PLA"))
+            a, b = v("PLA", 0, 18), v("PLB", 0, 18)
+            ts(a, v("IOD", 0, 18), v("PM"), A.add)
+            ts(b, a, -5.5, A.add, 1.0 / 12, A.mult)
+            ts(b, b, M23, A.add, M23, A.subtract)
+            ts(b, b, 4.0, A.mult)
+            tt(a, a, b, A.add)
+            cp(v("PLOUT"), a)
         for b in range(4):
             mm(4 + b, 128, "WQ", 128 * b, "LQ", 0, True, False)
             mm(4 + b, 128, "EBQ", 128 * b, "LQ", 0, False, True)
@@ -519,10 +497,118 @@ def rank_program(g, core, T, topo):
     act(v("QCS"), v("XQS"), off=v("PLOUT"))
     mm(0, C, "VQ", 0, "QC", 0)
     dmas([("s", T.oc[:, :], T.QC[:, :].bitcast(dt.uint8), [v("QC")], [])])
-    act(v("YO", 0, 144), ps(0, 144))
+    act(v("YO"), ps(0, C))
     dmas([("s" if k % 2 else "a", T.osc[4 * k:4 * k + 4, :], T.QCS[32 * k:32 * k + 4, :], [v("QCS")], []) for k in range(4)])
-    cp(v("YO", 144, 288), ps(0, 144, 144))
     dmas([("s", T.y[:, :], T.YO[:, :], [v("YO")], [])])
+
+    n = len(nodes)
+    pred = [dict() for _ in nodes]
+    hist = {}
+    for i, nd_ in enumerate(nodes):
+        if "after" in nd_:
+            pred[i][nd_["after"]] = True
+        for kind, accs in (("r", nd_["r"]), ("w", nd_["w"])):
+            for x in accs:
+                for (k2, x2, j) in hist.get(x[0], ()):
+                    same = nodes[j]["e"] == nd_["e"] and nodes[j]["kind"] == "c" and nd_["kind"] == "c"
+                    if j == i or (nd_["tok"] is not None and nodes[j]["tok"] == nd_["tok"]) or (kind == "r" and k2 == "r" and (same or x[0][:3] != "PS.")) or not meet(x, x2):
+                        continue
+                    done = not (same and x[0][:3] == "PS." and nd_["e"] == "p")
+                    pred[i][j] = pred[i].get(j, False) or done
+        for kind, accs in (("r", nd_["r"]), ("w", nd_["w"])):
+            for x in accs:
+                l = hist.setdefault(x[0], [])
+                if kind == "w":
+                    l[:] = [o for o in l if not covers(x, o[1]) or (nd_["tok"] is not None and nodes[o[2]]["tok"] == nd_["tok"])]
+                l.append((kind, x, i))
+    succ = [[] for _ in nodes]
+    left = [0] * n
+    for i in range(n):
+        left[i] = len(pred[i])
+        for j in pred[i]:
+            succ[j].append(i)
+    path = [0.0] * n
+    for i in range(n - 1, -1, -1):
+        best = 0.0
+        for j in succ[i]:
+            best = max(best, path[j] + ((nodes[i]["lat"] + WAKE) if pred[j][i] else 0.0))
+        path[i] = best + nodes[i]["dur"]
+    free = {e: 0.0 for e in Q}
+    end = [0.0] * n
+    est = [0.0] * n
+    ready = {e: [] for e in list(Q) + [None]}
+    for i in range(n):
+        if not left[i]:
+            ready[nodes[i]["e"]].append(i)
+    order = []
+    while len(order) < n:
+        pick = None
+        for e in ready:
+            l = ready[e]
+            if not l:
+                continue
+            f = free.get(e, 0.0)
+            first = min(max(f, est[i]) for i in l)
+            i = max((i for i in l if max(f, est[i]) <= first + DELTA), key=lambda i: path[i])
+            s = max(f, est[i])
+            if pick is None or s < pick[0]:
+                pick = (s, i, e)
+        s, i, e = pick
+        ready[e].remove(i)
+        order.append(i)
+        end[i] = s + nodes[i]["dur"]
+        if e is not None:
+            free[e] = end[i]
+        for j in succ[i]:
+            w = end[i] + nodes[i]["lat"] + (WAKE if nodes[j]["e"] is not None else 0.0) if pred[j][i] else s
+            est[j] = max(est[j], w)
+            left[j] -= 1
+            if not left[j]:
+                ready[nodes[j]["e"]].append(j)
+
+    recs = {}
+    for i in order:
+        x = nodes[i]
+        e, me = x["e"], (TOK.get(x["e"]) if x["kind"] == "c" else None)
+        tok = me if x["kind"] == "c" else x["tok"]
+        if e is not None:
+            need = {}
+            for kind, accs in (("r", x["r"]), ("w", x["w"])):
+                for y in accs:
+                    psum = y[0][:3] == "PS."
+                    for (k2, y2, tk, cnt, snap) in recs.get(y[0], ()):
+                        if kind == "r" and k2 == "r" and (tk == me or not psum):
+                            continue
+                        if tk == tok and x["kind"] == "d" or tk == me and psum and e == "p":
+                            continue
+                        if meet(y, y2) and know[e].get(tk, 0) < cnt and (tk not in need or need[tk][0] < cnt):
+                            need[tk] = (cnt, snap)
+            for tk in sorted(need, key=lambda q: (q == me, q)):
+                cnt, snap = need[tk]
+                if know[e].get(tk, 0) >= cnt or any(t2 != tk and s2[1].get(tk, 0) >= cnt and know[e].get(t2, 0) < s2[0] for t2, s2 in need.items()):
+                    continue
+                Q[e].wait_ge(T.sem[tk], cnt)
+                for t3, c3 in list(snap.items()) + [(tk, cnt)]:
+                    if know[e].get(t3, 0) < c3:
+                        know[e][t3] = c3
+        if x["kind"] == "c":
+            total[tok] += 1
+            x["fn"]().then_inc(T.sem[tok], 1)
+            cnt = total[tok]
+        else:
+            cnt = x["cnt"]
+            if x["kind"] == "d":
+                x["fn"]().then_inc(T.sem[tok], 16)
+            elif x["kind"] == "r":
+                x["fn"]()
+        snap = dict(know[e]) if e is not None else {}
+        snap[tok] = cnt
+        for kind, accs in (("r", x["r"]), ("w", x["w"])):
+            for y in accs:
+                l = recs.setdefault(y[0], [])
+                if kind == "w":
+                    l[:] = [o for o in l if not covers(y, o[1])]
+                l.append((kind, y, tok, cnt, snap))
     for tok in sorted(total):
         if total[tok]:
             g.wait_ge(T.sem[tok], total[tok])

@@ -1,7 +1,7 @@
 from concourse.bass import DstId, RemoteDMATransfer
 from concourse.mybir import dt, AluOpType, AxisListType, ActivationFunctionType
 
-N, C, R, NG = 8, 288, 3, 8
+C, R = 288, 3
 P = 384
 K = 96
 
@@ -12,16 +12,17 @@ def _b(name, cols, dtype, where="sbuf"):
     _S[name] = (where, [128, cols], dtype)
 
 
-for _n, _c in (("XN", 1152), ("XT", 1536), ("UT", 1024), ("VT", 512), ("FP", 3072), ("FO", 1536), ("TZ", 1920), ("ET", 512), ("BT", 1536), ("DT", 1536),
-               ("EB", 2048), ("TC", 1024), ("CW", 512), ("MC", 1088), ("WR", 384), ("H0", 384), ("H1", 384), ("NEG", 384), ("ONB", 128), ("ID", 128)):
+for _n, _c in (("XN", 1152), ("XT", 1536), ("UT", 1024), ("VT", 512), ("FP", 3072), ("GZ", 1536), ("TZ", 1920), ("ET", 512), ("BT", 1536), ("DT", 1536),
+               ("EB", 2048), ("TC", 1024), ("CW", 512), ("MC", 1088), ("WR", 384), ("H0", 384), ("H1", 384), ("NEG", 384),
+               ("PA0", 384), ("PA1", 384), ("NX0", 385), ("NX1", 385), ("ONB", 128), ("ID", 128)):
     _b(_n, _c, "bfloat16")
 for _n, _c in (("XNQ", 288), ("XQ", 384), ("QC", 288), ("UQ", 256), ("VQ", 128), ("EQ", 128), ("LQ", 128), ("BQ", 384), ("DQ", 384),
-               ("EBQ", 512), ("TCQ", 256), ("CWQ", 128), ("MCQ", 272), ("WQ", 512)):
+               ("EBQ", 512), ("EHQ", 512), ("TCQ", 256), ("CWQ", 128), ("MCQ", 272), ("WQ", 512)):
     _b(_n, _c, "float8_e4m3fn_x4")
     _b(_n + "S", _c, "uint8")
 for _n, _c in (("WI", 256), ("FLA", 256), ("FLB", 256), ("FLC", 256), ("NBT", 256), ("QROW", 384), ("MASK", 384), ("PADM", 384), ("NROW", 384), ("XH", 768),
-               ("PA0", 384), ("PA1", 384), ("NX0", 385), ("NX1", 385), ("HI", 1536), ("LO", 384), ("HH", 384), ("LO2", 192), ("HH2", 192), ("RG", 384), ("RMX", 384), ("RSC", 384),
-               ("D0G", 192), ("EN", 32), ("T1", 32), ("Y3", 96), ("L3", 96), ("LWW", 384), ("LMK", 96), ("LSC", 96), ("YO", 288), ("SC", 480)):
+               ("HI", 1536), ("LO", 384), ("HH", 384), ("LO2", 192), ("HH2", 192), ("RG", 384), ("RMX", 384), ("RSC", 384), ("D0G", 288), ("D0L", 96),
+               ("EN0", 32), ("EN1", 32), ("T10", 32), ("T11", 32), ("Y3", 96), ("L3", 96), ("LWW", 384), ("LMK", 96), ("LSC", 96), ("YO", 288), ("SC", 480)):
     _b(_n, _c, "float32")
 for _n, _c in (("DI", 48), ("XK", 384)):
     _b(_n, _c, "int32")
@@ -38,29 +39,29 @@ def _small(buf, names, w):
         _at[buf] += -(-w // 16) * 16
 
 
-_small("FC", "SEL8 ONE8 INV IM8 T8 T8B T8C", 8)
-_small("FC", "POW", 24)
+_small("FC", "SEL8 ONE8 INV IM8 T8 T8B T8C POW", 8)
 _small("FC", "WP IW IW2 IP0 IP1", 1)
-_small("FS", "GE PM PMC RC NRC NRK PML", 1)
-_small("FS", "IOA IOB IOC NC N96 N385 JC PADC BASE ONE24 BJ BQO BW RIF KEEP KB KU M0 M1 DROP KQ E1", 24)
+_small("FS", "GE PM PMC NRC NRX NRB PML", 1)
+_small("FS", "IOA IOB IOC NC N96 N513 JC PADC BASE ONE24 TWO BJ BQO BW RIF KEEP KBA KBB KUA KUB M0A M0B M1A M1B DROP KQ E1", 24)
 _small("FS", "EZ EU0 EU TS CD BK BD JD UU A1 A2 MNN PO SA SB SD SE AJA AJB AJC AJD PLA PLB IOD", 24)
-_small("FS", "PADV PADW RST XG ZZ VV VS KL VT2 KL2", 48)
-_small("FS", "D0R RM FD0 FD CI CX AJ AJT", 32)
+_small("FS", "CI", 33)
+_small("FS", "PADV RST XG ZZ VV VS KL VT2 KL2", 48)
+_small("FS", "D0R FD AJ AJT", 32)
 _small("FS", "Z16", 16)
-_small("FS", "W3", 3)
 for _n in _at:
     _b(_n, _at[_n], "float32")
-_b("D0L", 96, "float32")
 SCRATCH = _S
 SEMAPHORES = (["qv", "qa", "qp", "qg"] + ["d%d" % i for i in range(24)]
               + [n % t for t in range(R) for n in ("wr%d", "wl%d", "er%d", "el%d")])
 A = AluOpType
 ACT = ActivationFunctionType
 M23 = 1.5 * 2.0 ** 23
-M28 = 1.5 * 2.0 ** 28
+M19 = 1.5 * 2.0 ** 19
 CY = 0.00083
 WAKE = 0.15
-DELTA = 0.05
+DELTA = 0.03
+KA = 2
+KM = 2
 
 
 def rank_program(g, core, T, topo):
@@ -114,7 +115,6 @@ def rank_program(g, core, T, topo):
 
     def node(e, fn, reads, writes, dur, lat=0.0, tok=None, cnt=0, kind="c"):
         nodes.append({"e": e, "fn": fn, "r": [acc(x) for x in reads], "w": [acc(x) for x in writes], "dur": dur, "lat": lat, "tok": tok, "cnt": cnt, "kind": kind})
-        return len(nodes) - 1
 
     def dmas(items):
         tok = "d%d" % nd[0]
@@ -144,9 +144,6 @@ def rank_program(g, core, T, topo):
     def gath(off):
         return 0.05 + 16 * wid(off) * 1.56 * CY
 
-    def ttg(o, a, off, b, op):
-        node("v", lambda: g.vector.tensor_tensor(ap(o), ap(a).indirect(ap(off)), ap(b), op), [a, off, b], [o], gath(off))
-
     def cp(o, i):
         node("v", lambda: g.vector.tensor_copy(ap(o), ap(i)), [i], [o], cyc(wid(o) * half(o, i)))
 
@@ -164,7 +161,7 @@ def rank_program(g, core, T, topo):
 
     def scan(o, a, b, init, op0, op1):
         ini = ap(init) if isv(init) else init
-        node("v", lambda: g.vector.tensor_tensor_scan(ap(o), ap(a), ap(b), ini, op0, op1), [a, b] + ([init] if isv(init) else []), [o], cyc(wid(b)))
+        node("v", lambda: g.vector.tensor_tensor_scan(ap(o), ap(a), ap(b), ini, op0, op1), [a, b] + ([init] if isv(init) else []), [o], cyc(wid(b) * half(o, a, b)))
 
     def tr(o, i):
         node("v", lambda: g.vector.transpose(ap(o), ap(i)), [i], [o], cyc(wid(i)))
@@ -172,8 +169,8 @@ def rank_program(g, core, T, topo):
     def ms(o, c):
         node("v", lambda: g.vector.memset(ap(o), c), [], [o], cyc(wid(o) * half(o)))
 
-    def qz(q, i, lo=0, hi=None):
-        qv, sv = v(q, lo, hi), v(q + "S", lo, hi)
+    def qz(q, i):
+        qv, sv = v(q), v(q + "S")
         node("v", lambda: g.vector.quantize_mx(ap(qv), ap(sv), ap(i)), [i], [qv, sv], 0.012 + 0.00022 * wid(i))
 
     def act(o, i, scale=1.0, off=None):
@@ -186,8 +183,9 @@ def rank_program(g, core, T, topo):
         else:
             node("a", lambda: g.scalar.activation(ap(o), src(), ACT.Copy), rd, [o], d)
 
-    def actl(o, i, scale, bias):
-        node("a", lambda: g.scalar.activation(ap(o), ap(i), ACT.Identity, bias=bias, scale=scale), [i], [o], cyc(wid(i)))
+    def actl(o, i, scale, bias, relu=False):
+        bi = ap(bias) if isv(bias) else bias
+        node("a", lambda: g.scalar.activation(ap(o), ap(i), ACT.Relu if relu else ACT.Identity, bias=bi, scale=scale), [i] + ([bias] if isv(bias) else []), [o], cyc(wid(i)))
 
     def mm(bank, n, l, ll, r, rl, start=True, stop=True):
         o = v("PS", 512 * bank, 512 * bank + n)
@@ -200,19 +198,24 @@ def rank_program(g, core, T, topo):
     def asel(o, i, pat, op, fill, base, ch):
         node("g", lambda: g.affine_select(ap(o), ap(i), pat, op, fill, base, ch), [i], [o], 0.17 + 2 * wid(i) * CY)
 
-    def send(kind, t, parts, rd, calls, lands):
+    def send(kind, t, parts, rd, lands):
         lt, rt = kind + "l%d" % t, kind + "r%d" % t
-        n = neng * calls
+        n = neng * len(parts)
         total[lt] = total[rt] = n
 
         def fn():
             for (o, i) in parts:
                 g.remote_dma(o, i, T.sem[rt], T.sem[lt], pid, rid, mask)
-        node("g", fn, rd, [], 0.3 * calls, 1.5, lt, n, "r")
-        nodes.append({"e": None, "fn": None, "r": [], "w": [acc(x) for x in lands], "dur": 2.4 + 0.6 * (calls - 1), "lat": 0.0, "tok": rt, "cnt": n, "kind": "x", "after": len(nodes) - 1})
+        node("g", fn, rd, [], 0.3 * len(parts), 1.5, lt, n, "r")
+        nodes.append({"e": None, "fn": None, "r": [], "w": [acc(x) for x in lands], "dur": 1.8 + 0.6 * len(parts), "lat": 0.0, "tok": rt, "cnt": n, "kind": "x",
+                      "after": len(nodes) - 1})
 
-    def q24(k):
-        return 12 * (k // 4) + k % 4
+    def qs(k):
+        return (k, 18, 6) if k < 6 else (12 + k, 24, 2)
+
+    def qc(name, k, b):
+        lo, hi, st = qs(k)
+        return v(name, lo + st * b, lo + st * b + 1)
 
     dmas([("s", T.XN[:, 0:1152], T.x[:, :], [], [v("XN")])])
     dmas([("a", T.UT[:, 0:512], T.u[:, :], [], [v("UT", 0, 512)]), ("a", T.UT[:, 512:1024], T.u[:, :], [], [v("UT", 512, 1024)])])
@@ -241,12 +244,14 @@ def rank_program(g, core, T, topo):
     for e in (2, 3):
         ms(v("BT", e, 1536, 4), 0.0)
     for i in range(8):
-        ms(v("POW", i, 24, 8), 2.0 ** i)
+        ms(v("POW", i, i + 1), 2.0 ** i)
     ms(v("WOUT"), 0.0)
+    ms(v("TWO"), 2.0)
+    ms(v("TWO", 7, 24, 8), 0.0)
     ms(v("ET"), 0.0)
     qz("LQ", v("ET"))
-    node("v", lambda: g.vector.reciprocal(ap(v("INV")), ap(v("POW", 0, 8))), [v("POW", 0, 8)], [v("INV")], 0.25)
-    tt(v("T8B"), v("SEL8"), v("POW", 0, 8), A.mult)
+    node("v", lambda: g.vector.reciprocal(ap(v("INV")), ap(v("POW"))), [v("POW")], [v("INV")], 0.25)
+    tt(v("T8B"), v("SEL8"), v("POW"), A.mult)
     red(v("WP"), v("T8B"), A.add)
     tt(v("T8C"), v("SEL8"), v("INV"), A.mult)
     red(v("IW"), v("T8C"), A.add)
@@ -269,42 +274,41 @@ def rank_program(g, core, T, topo):
     cp(v("MC", 1025, 1056, 4), v("SEL8"))
     qz("MCQ", v("MC"))
     ms(v("EB"), 0.0)
-    for b in range(4):
-        act(v("EB", 512 * b + b, 512 * b + 512, 4), v("ID"), 32.0)
-    qz("EBQ", v("EB"))
+    for q, c in (("EHQ", 0.5), ("EBQ", 32.0)):
+        for b in range(4):
+            act(v("EB", 512 * b + b, 512 * b + 512, 4), v("ID"), c)
+        qz(q, v("EB"))
     ms(v("TC"), 0.0)
     for e in range(4):
         act(v("TC", 512 * (e // 2) + e, 512 * (e // 2) + 512, 4), v("ID"))
     qz("TCQ", v("TC"))
-    ms(v("NEG"), -1.0)
+    ms(v("NEG"), -1.0 / 512)
     ms(v("HI", 1520, 1536), 0.0)
-    ms(v("EN"), 0.0)
-    ms(v("Y3"), 0.0)
-    ms(v("AJ"), 0.0)
-    ms(v("Z16"), 0.0)
+    for n in ("EN0", "EN1", "KEEP", "Y3", "AJ", "Z16", "CI"):
+        ms(v(n), 0.0)
     ms(v("ONE24"), 1.0)
-    for n, w in (("D0R", 32), ("D0L", 96), ("D0G", 192)):
+    for n, w, f in (("D0R", 32, 15), ("D0L", 96, 0), ("D0G", 288, 0)):
         ms(v(n), 1.0)
-        ms(v(n, 0, w, 16), 0.0)
+        ms(v(n, f, w, 16), 0.0)
     ms(v("RST"), 0.0)
     ms(v("RST", 0, 48, 16), 2048.0)
     for k in range(8):
-        iota(v("BASE", q24(k), q24(k) + 9, 4), [[2 ** (8 - k), 3]], 3 * (512 - 2 ** (9 - k)) - (1440 if k > 3 else 0))
+        iota(v("BASE", *qs(k)), [[2 ** (8 - k), 3]], 3 * (512 - 2 ** (9 - k)) - (1512 if k > 5 else 0))
     iota(v("NROW"), [[1, P]])
     iota(v("IOB"), [[16, 24]])
     iota(v("IOC"), [[4, 24]], 276)
     iota(v("IOD", 0, 18), [[16, 18]])
     ts(v("PADM"), v("QROW"), 12.0, A.is_ge, 1000.0, A.mult)
     ts(v("NRC"), v("PM"), 12.0, A.is_ge)
-    ts(v("NRK"), v("NRC"), 1024.0, A.mult)
-    ts(v("PADW"), v("QROW", 0, 48), 12.0, A.is_ge, 1024.0, A.mult)
-    ts(v("PADV"), v("PADW"), v("NRK"), A.add)
+    ts(v("NRX"), v("NRC"), -5000.0, A.mult)
+    ts(v("NRB"), v("NRC"), -100000.0, A.mult)
+    ts(v("RST", 0, 48, 16), v("RST", 0, 48, 16), v("NRB"), A.add)
+    ts(v("PADV"), v("QROW", 0, 48), 12.0, A.is_ge, 1024.0, A.mult)
     ts(v("MASK"), v("QROW"), v("PM"), A.is_equal)
-    ts(v("RM"), v("QROW", 0, 32), 12.0, A.is_lt)
     ts(v("NC"), v("IOB"), v("PM"), A.add)
     ts(v("N96"), v("NC"), 96.0, A.add)
-    ts(v("N385"), v("NC"), 385.0, A.add)
-    ts(v("JC"), v("IOA"), v("PM"), A.add)
+    ts(v("N513"), v("NC"), 513.25, A.add)
+    ts(v("JC"), v("IOA"), v("PM"), A.add, v("NRX"), A.add)
     ts(v("PADC"), v("IOC"), v("PM"), A.add, v("NRC"), A.mult)
 
     def seg(k):
@@ -317,112 +321,112 @@ def rank_program(g, core, T, topo):
         mm(3, P, "UQ", u0, "XQ", 0)
         for b in range(3):
             ts(v("BJ", 8 * b, 8 * b + 8), ps(b, 128, 0, 16), 0.0, A.is_gt)
-        tt(v("BW"), v("BJ"), v("POW"), A.mult)
-        for b in range(3):
-            red(v("W3", b, b + 1), v("BW", 8 * b, 8 * b + 8), A.add)
-        for b in range(3):
-            ts(v("WOUT", 2 * b, 2 * b + 1), v("W3", b, b + 1), 0.0, A.add)
+        scan(v("BW", 0, 24, 1, True), v("TWO", 0, 24, 1, True), v("BJ", 0, 24, 1, True), 0.0, A.mult, A.add)
+        cp(v("WOUT", 0, 6, 2), v("BW", 0, 24, 8))
         lw = "LW%d" % t
-        send("w", t, [(T[lw][:, 0:6], T.WOUT[:, 0:6])], [v("WOUT")] + ([v("LQ"), v("LQS")] if t == 0 else []), 1, [v(lw)])
+        send("w", t, [(T[lw][:, 0:6], T.WOUT[:, 0:6])], [v("WOUT")] + ([v("LQ"), v("LQS")] if t == 0 else []), [v(lw)])
         for b in range(3):
-            for h in range(2):
-                cp(v("BQO", 12 * h + 4 * b, 12 * h + 4 * b + 4), v("BJ", 8 * b + 4 * h, 8 * b + 4 * h + 4))
+            for q, k, n in ((6 * b, 0, 6), (18 + 2 * b, 6, 2)):
+                act(v("BQO", q, q + n), v("BJ", 8 * b + k, 8 * b + k + n))
         ts(v("BT", 0, 1536, 4), ps(3, P), 0.0, A.is_gt)
-        actl(v("BT", 1, 1536, 4), v("BT", 0, 1536, 4), -1.0, 1.0)
+        ts(v("BT", 1, 1536, 4), ps(3, P), 0.0, A.is_le)
         qz("BQ", v("BT"))
         mm(3, P, "CWQ", 0, "BQ", 0)
+        wrow = len(nodes) - 1
         for b in range(3):
             mm(b, 272, "BQ", 128 * b, "MCQ", 0)
             act(v("XH", 256 * b, 256 * b + 256), ps(b, 256), 0.5)
-            for h in range(2):
-                q = 12 * h + 4 * b
-                tt(v("RIF", q, q + 4), ps(b, 4, 256 + 4 * h), v("BASE", q, q + 4), A.add)
+            for q, k, n in ((6 * b, 0, 6), (18 + 2 * b, 6, 2)):
+                tt(v("RIF", q, q + n), ps(b, n, 256 + k), v("BASE", q, q + n), A.add)
         cp(v("RI"), v("RIF"))
         tt(v("WR"), ps(3, P), v("PADM"), A.max)
         for h in range(2):
-            ts(v("H%d" % h), v("WR"), v("IP%d" % h), A.is_equal, float(P), A.mult)
-            scan(v("PA%d" % h, 0, P, 1, True), v("NEG"), v("H%d" % h, 0, P, 1, True), 0.0, A.add, A.max)
+            ts(v("H%d" % h), v("WR"), v("IP%d" % h), A.is_equal, 0.5, A.subtract)
+            scan(v("PA%d" % h, 0, P, 1, True), v("NEG"), v("H%d" % h, 0, P, 1, True), -0.5, A.add, A.max)
             scan(v("NX%d" % h, 0, P, 1, True), v("NEG"), v("H%d" % h, 0, P, 1, True), v("PA%d" % h, 0, 1), A.add, A.max)
             cp(v("NX%d" % h, P, P + 1), v("PA%d" % h, 0, 1))
-            ts(v("DT", 2 * h, 1536, 4), v("NX%d" % h, 1, P + 1), M28, A.add, M28, A.subtract)
+            ts(v("DT", 2 * h, 1536, 4), v("NX%d" % h, 1, P + 1), M19, A.add, M19, A.subtract)
             tt(v("DT", 2 * h + 1, 1536, 4), v("NX%d" % h, 1, P + 1), v("DT", 2 * h, 1536, 4), A.subtract)
         qz("DQ", v("DT"))
         for b in range(3):
             mm(b, 256, "DQ", 128 * b, "TCQ", 0)
-            act(v("HI", 256 * b, 256 * b + 256), ps(b, 256))
+            actl(v("HI", 256 * b, 256 * b + 256), ps(b, 256), 512.0, 256.0)
         for b in range(4):
-            mm(4 + b, P, "EBQ", 128 * b, "XQ", 0)
-            act(v("FP", 768 * b, 768 * b + P), ps(4 + b, P), 1.0 / 64)
-            act(v("FP", 768 * b + P, 768 * b + 768), ps(4 + b, P), 1.0 / 64)
-            act(v("FO", P * b, P * b + P), ps(4 + b, P), 1.0 / 64)
+            mm(4 + b, P, "EHQ", 128 * b, "XQ", 0)
+            nodes[-1]["behind"] = wrow
+            act(v("FP", 768 * b, 768 * b + P), ps(4 + b, P))
+            act(v("FP", 768 * b + P, 768 * b + 768), ps(4 + b, P))
         for b in range(3):
             cpg(v("XG", 16 * b, 16 * b + 16), v("XH", 256 * b, 256 * b + 256), v(lw, 2 * b, 2 * b + 1))
         ts(v("ZZ"), v("XG"), 0.0, A.is_equal, 1024.0, A.mult)
         tt(v("VV"), v("XG"), v("PADV"), A.add)
         tt(v("VV"), v("VV"), v("ZZ"), A.max)
         ts(v("DI"), v("XG"), 2.0, A.mult)
-        for k in range(8):
-            if k < 7:
-                ts(v("XK", 48 * k, 48 * k + 48), v("DI"), 1 << k, A.bitwise_and)
+        for k in range(7):
+            ts(v("XK", 48 * k, 48 * k + 48), v("DI"), 1 << k, A.bitwise_and)
         for k in range(8):
             vs, kl = ("VS", "KL") if k % 2 else ("VT2", "KL2")
             scan(v(vs), v("RST"), v("VV"), 4096.0, A.add, A.min)
             for b in range(3):
                 if k < 7:
                     ts(v(kl, 16 * b, 16 * b + 16), v("XK", 48 * k + 16 * b, 48 * k + 16 * b + 16), v(vs, 16 * b + 15, 16 * b + 16), A.is_gt, 4096.0, A.mult)
-            ts(v("KEEP", q24(k), q24(k) + 9, 4), v(vs, 15, 48, 16), float(1 << k), A.is_lt)
+            ts(v("KEEP", *qs(k)), v(vs, 15, 48, 16), float(1 << k), A.is_lt)
             if k < 7:
                 tt(v("VV"), v("VV"), v(kl), A.max)
-            if k % 4 == 3:
-                lo, hi = 3 * k - 9, 3 * k + 3
-                tt(v("KB", lo, hi), v("KEEP", lo, hi), v("BQO", lo, hi), A.mult)
-                ts(v("M0", lo, hi), v("KB", lo, hi), -1.0, A.mult, 1.0, A.add)
-                tt(v("KU", lo, hi), v("KB", lo, hi), v("KEEP", lo, hi), A.subtract)
-                ts(v("M1", lo, hi), v("KU", lo, hi), 1.0, A.add)
-                ts(v("DROP", lo, hi), v("KEEP", lo, hi), -1.0, A.mult, 1.0, A.add)
-                ts(v("KQ", lo, hi), v("KEEP", lo, hi), 0.25, A.mult)
+            if k in (KM, 5, 6):
+                (lo, hi), s = ((0, 18) if k < 6 else (18, 24)), ("A" if k == KM else "B")
+                tt(v("KB" + s, lo, hi), v("KEEP", lo, hi), v("BQO", lo, hi), A.mult)
+                actl(v("M0" + s, lo, hi), v("KB" + s, lo, hi), -1.0, 1.0)
+                tt(v("KU" + s, lo, hi), v("KB" + s, lo, hi), v("KEEP", lo, hi), A.subtract)
+                actl(v("M1" + s, lo, hi), v("KU" + s, lo, hi), 1.0, 1.0)
+            if k in (5, 7):
+                lo, hi = (0, 18) if k < 6 else (18, 24)
+                actl(v("DROP", lo, hi), v("KEEP", lo, hi), -1.0, 1.0)
+                act(v("KQ", lo, hi), v("KEEP", lo, hi), 0.0625)
         for k in range(8):
             if k < 7:
                 n, s0 = 2 ** (7 - k), seg(k)
-                lo, hh = ("LO2", "HH2") if k % 2 else ("LO", "HH")
+                l_, h_ = ("LO2", "HH2") if k % 2 else ("LO", "HH")
                 for b in range(3):
-                    s, m = s0 + 2 * n * b, q24(k) + 4 * b
-                    act(v(hh, n * b, n * b + n), v("HI", s + 1, s + 2 * n, 2), v("M1", m, m + 1))
-                    ts(v(lo, n * b, n * b + n), v("HI", s, s + 2 * n, 2), v("M0", m, m + 1), A.mult)
-                tt(v("HI", seg(k + 1), seg(k + 1) + 3 * n), v(lo, 0, 3 * n), v(hh, 0, 3 * n), A.max)
-            if k % 4 == 3:
-                h = k // 4
-                o = 192 * h
-                cpg(v("RG", o, o + 192), v("HI", 1440 * h, 1440 + 96 * h), v("RI", 12 * h, 12 * h + 12))
-                tt(v("RMX", o, o + 192), v("RG", o, o + 192), v("MASK", 0, 192), A.mult)
-                scan(v("RSC", o, o + 192), v("D0G"), v("RMX", o, o + 192), 0.0, A.mult, A.max)
-                tt(v("E1", 12 * h, 12 * h + 12), v("RSC", o + 15, o + 192, 16), v("DROP", 12 * h, 12 * h + 12), A.mult)
-                tt(v("EN", 12 * h, 12 * h + 12), v("E1", 12 * h, 12 * h + 12), v("KQ", 12 * h, 12 * h + 12), A.subtract)
-        tr(v("T1"), v("EN"))
-        items = []
-        for k in range(8):
-            gr = (3 * t + k) % 8
-            for b in range(3):
-                p0, c0 = 32 * (gr // 2) + 8 * b, 16 * (gr % 2)
-                items.append(("s" if (3 * k + b) % 2 else "a", T.Y3[p0:p0 + 8, c0:c0 + 16], T.T1[q24(k) + 4 * b::32, 0:32], [v("T1")], [v("Y3", c0, c0 + 16)]))
-        dmas(items)
+                    s, m = s0 + 2 * n * b, "A" if k <= KM else "B"
+                    act(v(h_, n * b, n * b + n), v("HI", s + 1, s + 2 * n, 2), qc("M1" + m, k, b))
+                    if k < KA:
+                        act(v(l_, n * b, n * b + n), v("HI", s, s + 2 * n, 2), qc("M0" + m, k, b))
+                    else:
+                        ts(v(l_, n * b, n * b + n), v("HI", s, s + 2 * n, 2), qc("M0" + m, k, b), A.mult)
+                tt(v("HI", seg(k + 1), seg(k + 1) + 3 * n), v(l_, 0, 3 * n), v(h_, 0, 3 * n), A.max)
+            if k in (5, 7):
+                h, lo, hi = (0, 0, 18) if k == 5 else (1, 18, 24)
+                o, n = 16 * lo, 16 * (hi - lo)
+                cpg(v("RG", o, o + n), v("HI", 1512 * h, 1512 + 24 * h), v("RI", lo, hi))
+                tt(v("RMX", o, o + n), v("RG", o, o + n), v("MASK", 0, n), A.mult)
+                scan(v("RSC", o, o + n), v("D0G", 0, n), v("RMX", o, o + n), 0.0, A.mult, A.max)
+                tt(v("E1", lo, hi), v("RSC", o + 15, o + n, 16), v("DROP", lo, hi), A.mult)
+                tt(v("EN%d" % h, 0, hi - lo), v("E1", lo, hi), v("KQ", lo, hi), A.subtract)
+                tr(v("T1%d" % h), v("EN%d" % h))
+                items = []
+                for kk in (range(6) if h == 0 else (6, 7)):
+                    gr = (3 * t + kk) % 8
+                    for b in range(3):
+                        p0, c0 = 32 * (gr // 2) + 8 * b, 16 * (gr % 2)
+                        x = 6 * b + kk if h == 0 else 2 * b + kk - 6
+                        items.append(("s" if (kk + b) % 2 else "a", T.Y3[p0:p0 + 8, c0:c0 + 16], T["T1%d" % h][x::32, 0:32], [v("T1%d" % h)], [v("Y3", c0, c0 + 16)]))
+                dmas(items)
         tr(v("L3", 0, 32), v("Y3", 0, 32))
         e = v("L3", 0, 24)
-        ts(v("EZ"), e, 0.0, A.is_le, 385.0, A.mult)
-        tt(v("EU0"), v("N385"), e, A.subtract)
+        actl(v("EZ"), e, -4.01, 513.0, True)
+        tt(v("EU0"), v("N513"), e, A.subtract)
         tt(v("EU"), v("EU0"), v("EZ"), A.subtract)
         cp(v("AL"), v("EU"))
-        ts(v("FD0"), v("Y3", 0, 32), 0.0, A.is_ge)
-        tt(v("FD"), v("FD0"), v("RM"), A.mult)
-        scan(v("CI"), v("D0R"), v("FD"), 0.0, A.mult, A.add)
-        tt(v("CX"), v("CI"), v("FD"), A.subtract)
+        ts(v("FD"), v("Y3", 0, 32), 0.0, A.is_ge)
+        scan(v("CI", 1, 33), v("D0R"), v("FD"), 0.0, A.mult, A.add)
         for h in range(2):
             last = v("CI", 16 * h + 15, 16 * h + 16)
-            ts(v("Y3", 32 + 16 * h, 48 + 16 * h), v("CX", 16 * h, 16 * h + 16), last, A.subtract)
-            ts(v("Y3", 64 + 16 * h, 80 + 16 * h), v("Z16"), last, A.add)
+            ts(v("Y3", 32 + 16 * h, 48 + 16 * h), v("CI", 16 * h, 16 * h + 16), last, A.subtract)
+            actl(v("Y3", 64 + 16 * h, 80 + 16 * h), v("Z16"), 1.0, last)
         tr(v("L3", 32, 96), v("Y3", 32, 96))
-        ts(v("BK"), e, 0.0, A.is_lt, 4096.0, A.mult)
-        ts(v("BD"), e, 0.0, A.is_ge, 4096.0, A.mult)
+        actl(v("BK"), e, -65536.0, 0.0, True)
+        actl(v("BD"), v("BK"), -1.0, 4096.0)
         tt(v("JD"), v("JC"), v("BD"), A.add)
         scan(v("TS"), v("ONE24"), v("L3", 64, 88), 0.0, A.mult, A.add)
         tt(v("CD"), v("L3", 32, 56), v("TS"), A.add)
@@ -437,7 +441,8 @@ def rank_program(g, core, T, topo):
         scan(v("LSC"), v("D0L"), v("LMK"), 0.0, A.mult, A.add)
         cp(v("L6U"), v("LSC", 15, K, 16))
         for b in range(4):
-            ttg(v("TZ", 480 * b + K, 480 * b + 480), v("FP", 768 * b, 768 * b + 768), v("AL"), v("FO", P * b, P * b + P), A.add)
+            act(v("GZ", P * b, P * b + P), v("FP", 768 * b, 768 * b + 768), off=v("AL"))
+            tt(v("TZ", 480 * b + K, 480 * b + 480), v("GZ", P * b, P * b + P), ps(4 + b, P), A.add)
         for b in range(4):
             z, o = v("TZ", 480 * b + K, 480 * b + 480), v("ET", b, 4 * K, 4)
             if b % 2:
@@ -446,7 +451,7 @@ def rank_program(g, core, T, topo):
                 act(o, z, off=v("L6U"))
         qz("EQ", v("ET"))
         send("e", t, [(T.LQ[:, 0:K].bitcast(dt.uint8), T.EQ[:, 0:K].bitcast(dt.uint8)), (T.LQS[:, 0:K], T.EQS[:, 0:K])],
-             [v("EQ"), v("EQS")], 2, [v("LQ", 0, K), v("LQS", 0, K)])
+             [v("EQ"), v("EQS")], [v("LQ", 0, K), v("LQS", 0, K)])
         ts(v("SA"), v("PO"), float(K), A.is_lt)
         tt(v("SB"), v("PO"), v("N96"), A.subtract)
         tt(v("SD"), v("SA"), v("SB"), A.mult)
@@ -504,22 +509,28 @@ def rank_program(g, core, T, topo):
     n = len(nodes)
     pred = [dict() for _ in nodes]
     hist = {}
-    for i, nd_ in enumerate(nodes):
-        if "after" in nd_:
-            pred[i][nd_["after"]] = True
-        for kind, accs in (("r", nd_["r"]), ("w", nd_["w"])):
+    for i, nw in enumerate(nodes):
+        if "after" in nw:
+            pred[i][nw["after"]] = True
+        if "behind" in nw:
+            pred[i][nw["behind"]] = False
+        for kind, accs in (("r", nw["r"]), ("w", nw["w"])):
             for x in accs:
                 for (k2, x2, j) in hist.get(x[0], ()):
-                    same = nodes[j]["e"] == nd_["e"] and nodes[j]["kind"] == "c" and nd_["kind"] == "c"
-                    if j == i or (nd_["tok"] is not None and nodes[j]["tok"] == nd_["tok"]) or (kind == "r" and k2 == "r" and (same or x[0][:3] != "PS.")) or not meet(x, x2):
+                    od = nodes[j]
+                    both = nw["kind"] == "d" and od["kind"] == "d"
+                    if j == i or (both and (x[0] == "Y3" or od["tok"] == nw["tok"])):
                         continue
-                    done = not (same and x[0][:3] == "PS." and nd_["e"] == "p")
+                    same = od["e"] == nw["e"] and od["kind"] == "c" and nw["kind"] == "c"
+                    if (kind == "r" and k2 == "r" and (same or x[0][:3] != "PS.")) or not meet(x, x2):
+                        continue
+                    done = not (same and x[0][:3] == "PS." and nw["e"] == "p")
                     pred[i][j] = pred[i].get(j, False) or done
-        for kind, accs in (("r", nd_["r"]), ("w", nd_["w"])):
+        for kind, accs in (("r", nw["r"]), ("w", nw["w"])):
             for x in accs:
                 l = hist.setdefault(x[0], [])
                 if kind == "w":
-                    l[:] = [o for o in l if not covers(x, o[1]) or (nd_["tok"] is not None and nodes[o[2]]["tok"] == nd_["tok"])]
+                    l[:] = [o for o in l if not covers(x, o[1]) or (nw["kind"] == "d" and nodes[o[2]]["kind"] == "d")]
                 l.append((kind, x, i))
     succ = [[] for _ in nodes]
     left = [0] * n
@@ -534,7 +545,6 @@ def rank_program(g, core, T, topo):
             best = max(best, path[j] + ((nodes[i]["lat"] + WAKE) if pred[j][i] else 0.0))
         path[i] = best + nodes[i]["dur"]
     free = {e: 0.0 for e in Q}
-    end = [0.0] * n
     est = [0.0] * n
     ready = {e: [] for e in list(Q) + [None]}
     for i in range(n):
@@ -556,11 +566,11 @@ def rank_program(g, core, T, topo):
         s, i, e = pick
         ready[e].remove(i)
         order.append(i)
-        end[i] = s + nodes[i]["dur"]
+        end = s + nodes[i]["dur"]
         if e is not None:
-            free[e] = end[i]
+            free[e] = end
         for j in succ[i]:
-            w = end[i] + nodes[i]["lat"] + (WAKE if nodes[j]["e"] is not None else 0.0) if pred[j][i] else s
+            w = end + nodes[i]["lat"] + (WAKE if nodes[j]["e"] is not None else 0.0) if pred[j][i] else s
             est[j] = max(est[j], w)
             left[j] -= 1
             if not left[j]:
@@ -579,7 +589,7 @@ def rank_program(g, core, T, topo):
                     for (k2, y2, tk, cnt, snap) in recs.get(y[0], ()):
                         if kind == "r" and k2 == "r" and (tk == me or not psum):
                             continue
-                        if tk == tok and x["kind"] == "d" or tk == me and psum and e == "p":
+                        if x["kind"] == "d" and (tk == tok or tk[0] == "d" and y[0] == "Y3") or tk == me and psum and e == "p":
                             continue
                         if meet(y, y2) and know[e].get(tk, 0) < cnt and (tk not in need or need[tk][0] < cnt):
                             need[tk] = (cnt, snap)
@@ -607,7 +617,7 @@ def rank_program(g, core, T, topo):
             for y in accs:
                 l = recs.setdefault(y[0], [])
                 if kind == "w":
-                    l[:] = [o for o in l if not covers(y, o[1])]
+                    l[:] = [o for o in l if not covers(y, o[1]) or (x["kind"] == "d" and o[2][0] == "d")]
                 l.append((kind, y, tok, cnt, snap))
     for tok in sorted(total):
         if total[tok]:

from concourse.bass import DstId, RemoteDMATransfer
from concourse.mybir import dt, AluOpType, AxisListType, ActivationFunctionType

C, R = 288, 3
P = 384
K = 96

_S = {}


def _b(name, cols, dtype, where="sbuf"):
    _S[name] = (where, [128, cols], dtype)


for _n, _c in (("XN", 1152), ("XT", 1536), ("UT", 1024), ("VT", 512), ("FP", 3072), ("GZ", 1536), ("TZ", 1920), ("ET", 512), ("BT", 1536), ("DT", 1536),
               ("EB", 2048), ("TC", 1024), ("CW", 512), ("MC", 1088), ("WR", 384), ("H0", 384), ("H1", 384), ("NEG", 384),
               ("PA0", 384), ("PA1", 384), ("NX0", 385), ("NX1", 385), ("ONB", 128), ("ID", 128)):
    _b(_n, _c, "bfloat16")
for _n, _c in (("XNQ", 288), ("XQ", 384), ("QC", 288), ("UQ", 256), ("VQ", 128), ("EQ", 128), ("LQ", 128), ("BQ", 384), ("DQ", 384),
               ("EBQ", 512), ("EHQ", 512), ("TCQ", 256), ("CWQ", 128), ("MCQ", 272), ("WQ", 512)):
    _b(_n, _c, "float8_e4m3fn_x4")
    _b(_n + "S", _c, "uint8")
for _n, _c in (("WI", 256), ("FLA", 256), ("FLB", 256), ("FLC", 256), ("NBT", 256), ("QROW", 384), ("MASK", 384), ("PADM", 384), ("NROW", 384), ("XH", 768),
               ("HI", 1536), ("LO", 384), ("HH", 384), ("LO2", 192), ("HH2", 192), ("RG", 384), ("RMX", 384), ("RSC", 384), ("D0G", 288), ("D0L", 96),
               ("EN0", 32), ("EN1", 32), ("T10", 32), ("T11", 32), ("Y3", 96), ("L3", 96), ("LWW", 384), ("LMK", 96), ("LSC", 96), ("YO", 288), ("SC", 480)):
    _b(_n, _c, "float32")
for _n, _c in (("DI", 48), ("XK", 384)):
    _b(_n, _c, "int32")
for _n, _c in (("WOUT", 6), ("LW0", 6), ("LW1", 6), ("LW2", 6), ("RI", 24), ("AL", 24), ("PL", 24), ("SL", 24), ("L6U", 6), ("PLIN", 24), ("PLOUT", 18)):
    _b(_n, _c, "uint16")
_b("PS", 4096, "float32", "psum")
_SMALL, _WID, _at = {}, {}, {"FC": 0, "FS": 0}


def _small(buf, names, w):
    for n in names.split():
        _SMALL[n] = (buf, _at[buf])
        _WID[n] = w
        _at[buf] += -(-w // 16) * 16


_small("FC", "SEL8 ONE8 INV IM8 T8 T8B T8C POW", 8)
_small("FC", "WP IW IW2 IP0 IP1", 1)
_small("FS", "GE PM PMC NRC NRX NRB PML", 1)
_small("FS", "IOA IOB IOC NC N96 N513 JC PADC BASE ONE24 TWO BJ BQO BW RIF KEEP KBA KBB KUA KUB M0A M0B M1A M1B DROP KQ E1", 24)
_small("FS", "EZ EU0 EU TS CD BK BD JD UU A1 A2 MNN PO SA SB SD SE AJA AJB AJC AJD PLA PLB IOD", 24)
_small("FS", "CI", 33)
_small("FS", "PADV RST XG ZZ VV VS KL VT2 KL2", 48)
_small("FS", "D0R FD AJ AJT", 32)
_small("FS", "Z16", 16)
for _n in _at:
    _b(_n, _at[_n], "float32")
SCRATCH = _S
SEMAPHORES = (["qv", "qa", "qp", "qg"] + ["d%d" % i for i in range(24)]
              + [n % t for t in range(R) for n in ("wr%d", "wl%d", "er%d", "el%d")])
A = AluOpType
ACT = ActivationFunctionType
M23 = 1.5 * 2.0 ** 23
M19 = 1.5 * 2.0 ** 19
CY = 0.00083
WAKE = 0.15
DELTA = 0.03
KA = 2
KM = 2


def rank_program(g, core, T, topo):
    rank = T.rank_of(core)
    if rank is None:
        return
    mate = T.cores[rank ^ 1]
    rid, pid = topo.addr(mate, core)
    mask = topo.mask(core, mate)
    neng = len(topo.engines(core, mate))
    Q = {"v": g.vector, "a": g.scalar, "p": g.tensor, "g": g, "s": g.sync}
    TOK = {"v": "qv", "a": "qa", "p": "qp", "g": "qg"}
    total = {k: 0 for k in ("qv", "qa", "qp", "qg")}
    know = {e: {} for e in Q}
    nodes = []
    nd = [0]

    def v(name, lo=0, hi=None, st=1, rev=False):
        if name in _SMALL:
            buf, o = _SMALL[name]
            return (buf, o + lo, o + (_WID[name] if hi is None else hi), st, rev)
        return (name, lo, SCRATCH[name][1][1] if hi is None else hi, st, rev)

    def ps(bank, n, lo=0, st=1):
        return v("PS", 512 * bank + lo, 512 * bank + lo + n, st)

    def ap(w):
        t = T[w[0]]
        if w[4]:
            return t[:, w[2] - 1:(w[1] - 1 if w[1] > 0 else None):-1]
        return t[:, w[1]:w[2]] if w[3] == 1 else t[:, w[1]:w[2]:w[3]]

    def wid(w):
        return len(range(w[1], w[2], w[3]))

    def half(*ws):
        return 0.5 if all(SCRATCH[w[0]][2] in ("bfloat16", "uint16") for w in ws) else 1.0

    def acc(w):
        if w[0] == "PS":
            return ("PS.%d" % (w[1] // 512), 0, 1, 1)
        return w[:4]

    def meet(a, b):
        if a[1] >= b[2] or b[1] >= a[2]:
            return False
        return not (a[3] == b[3] and a[3] > 1 and (a[1] - b[1]) % a[3])

    def covers(x, y):
        return x[1] <= y[1] and x[2] >= y[2] and (x[3] == 1 or (x[3] == y[3] and (x[1] - y[1]) % x[3] == 0))

    def node(e, fn, reads, writes, dur, lat=0.0, tok=None, cnt=0, kind="c"):
        nodes.append({"e": e, "fn": fn, "r": [acc(x) for x in reads], "w": [acc(x) for x in writes], "dur": dur, "lat": lat, "tok": tok, "cnt": cnt, "kind": kind})

    def dmas(items):
        tok = "d%d" % nd[0]
        nd[0] += 1
        total[tok] = 16 * len(items)
        for (e, o, i, rd, wr) in items:
            node(e, (lambda e=e, o=o, i=i: Q[e].dma_start(o, i)), rd, wr, 0.07, 2.0, tok, total[tok], "d")

    def isv(x):
        return x is not None and not isinstance(x, (int, float))

    def cyc(n):
        return max(64, n) * CY

    def ts(o, i, s1, op0, s2=None, op1=None):
        a1, a2 = (ap(s1) if isv(s1) else s1), (ap(s2) if isv(s2) else s2)
        rd = [i] + [x for x in (s1, s2) if isv(x)]
        d = cyc(wid(o) * half(o, i))
        if op1 is None:
            node("v", lambda: g.vector.tensor_scalar(ap(o), ap(i), a1, None, op0), rd, [o], d)
        else:
            node("v", lambda: g.vector.tensor_scalar(ap(o), ap(i), a1, a2, op0, op1), rd, [o], d)

    def tt(o, a, b, op):
        node("v", lambda: g.vector.tensor_tensor(ap(o), ap(a), ap(b), op), [a, b], [o], cyc(wid(o) * (1 if "PS" in (a[0], b[0]) else 2)))

    def gath(off):
        return 0.05 + 16 * wid(off) * 1.56 * CY

    def cp(o, i):
        node("v", lambda: g.vector.tensor_copy(ap(o), ap(i)), [i], [o], cyc(wid(o) * half(o, i)))

    def cpg(o, i, off):
        node("v", lambda: g.vector.tensor_copy(ap(o), ap(i).indirect(ap(off))), [i, off], [o], gath(off))

    def scat(o, off, i):
        node("v", lambda: g.vector.tensor_copy(ap(o).indirect(ap(off)), ap(i)), [i, off], [o], 0.05 + 3 * wid(i) * CY)

    def pickc(o, i, off):
        node("v", lambda: g.vector.tensor_copy(ap(o).bitcast(dt.uint32), ap(i).bitcast(dt.uint32).indirect(ap(off))), [i, off], [o], gath(off))

    def red(o, i, op):
        node("v", lambda: g.vector.tensor_reduce(ap(o), ap(i), AxisListType.X, op), [i], [o], cyc(wid(i)))

    def scan(o, a, b, init, op0, op1):
        ini = ap(init) if isv(init) else init
        node("v", lambda: g.vector.tensor_tensor_scan(ap(o), ap(a), ap(b), ini, op0, op1), [a, b] + ([init] if isv(init) else []), [o], cyc(wid(b) * half(o, a, b)))

    def tr(o, i):
        node("v", lambda: g.vector.transpose(ap(o), ap(i)), [i], [o], cyc(wid(i)))

    def ms(o, c):
        node("v", lambda: g.vector.memset(ap(o), c), [], [o], cyc(wid(o) * half(o)))

    def qz(q, i):
        qv, sv = v(q), v(q + "S")
        node("v", lambda: g.vector.quantize_mx(ap(qv), ap(sv), ap(i)), [i], [qv, sv], 0.012 + 0.00022 * wid(i))

    def act(o, i, scale=1.0, off=None):
        sc = ap(scale) if isv(scale) else scale
        rd = [i] + ([scale] if isv(scale) else []) + ([off] if off is not None else [])
        src = (lambda: ap(i).indirect(ap(off))) if off is not None else (lambda: ap(i))
        d = 0.015 + gath(off) if off is not None else cyc(wid(i))
        if isv(scale) or scale != 1.0:
            node("a", lambda: g.scalar.activation(ap(o), src(), ACT.Copy, scale=sc), rd, [o], d)
        else:
            node("a", lambda: g.scalar.activation(ap(o), src(), ACT.Copy), rd, [o], d)

    def actl(o, i, scale, bias, relu=False):
        bi = ap(bias) if isv(bias) else bias
        node("a", lambda: g.scalar.activation(ap(o), ap(i), ACT.Relu if relu else ACT.Identity, bias=bi, scale=scale), [i] + ([bias] if isv(bias) else []), [o], cyc(wid(i)))

    def mm(bank, n, l, ll, r, rl, start=True, stop=True):
        o = v("PS", 512 * bank, 512 * bank + n)
        lq, ls, rq, rs = v(l, ll, ll + 128), v(l + "S", ll, ll + 128), v(r, rl, rl + n), v(r + "S", rl, rl + n)
        node("p", lambda: g.tensor.matmul_mx(ap(o), ap(lq), ap(ls), ap(rq), ap(rs), start, stop), [lq, ls, rq, rs], [o], (n + 16) * CY * 1.2)

    def iota(o, pat, base=0, ch=0):
        node("g", lambda: g.iota(ap(o), pat, base, ch, allow_small_or_imprecise_dtypes=True), [], [o], 0.13 + 2 * wid(o) * CY)

    def asel(o, i, pat, op, fill, base, ch):
        node("g", lambda: g.affine_select(ap(o), ap(i), pat, op, fill, base, ch), [i], [o], 0.17 + 2 * wid(i) * CY)

    def send(kind, t, parts, rd, lands):
        lt, rt = kind + "l%d" % t, kind + "r%d" % t
        n = neng * len(parts)
        total[lt] = total[rt] = n

        def fn():
            for (o, i) in parts:
                g.remote_dma(o, i, T.sem[rt], T.sem[lt], pid, rid, mask)
        node("g", fn, rd, [], 0.3 * len(parts), 1.5, lt, n, "r")
        nodes.append({"e": None, "fn": None, "r": [], "w": [acc(x) for x in lands], "dur": 1.8 + 0.6 * len(parts), "lat": 0.0, "tok": rt, "cnt": n, "kind": "x",
                      "after": len(nodes) - 1})

    def qs(k):
        return (k, 18, 6) if k < 6 else (12 + k, 24, 2)

    def qc(name, k, b):
        lo, hi, st = qs(k)
        return v(name, lo + st * b, lo + st * b + 1)

    dmas([("s", T.XN[:, 0:1152], T.x[:, :], [], [v("XN")])])
    dmas([("a", T.UT[:, 0:512], T.u[:, :], [], [v("UT", 0, 512)]), ("a", T.UT[:, 512:1024], T.u[:, :], [], [v("UT", 512, 1024)])])
    dmas([("s", T.WQ[:, :].bitcast(dt.uint8), T.wc[:, :], [], [v("WQ")]), ("s", T.WQS[:, :], T.ws[:, :], [], [v("WQS")])])
    dmas([("s", T.VT[:, :], T.v[:, :], [], [v("VT")])])

    ms(v("ONE8"), 1.0)
    ms(v("ONB"), 1.0)
    iota(v("IP0"), [[0, 1]], 0, 1)
    asel(v("T8"), v("ONE8"), [[-16, 8]], A.is_ge, 0.0, 0, 1)
    iota(v("IOA"), [[12, 24]])
    asel(v("SEL8"), v("ONE8"), [[-16, 8]], A.is_equal, 0.0, 0, 1)
    iota(v("WI"), [[1, 256]])
    asel(v("ID"), v("ONB"), [[-1, 128]], A.is_equal, 0.0, 0, 1)
    iota(v("QROW"), [[0, 24], [1, 16]])
    iota(v("IP1"), [[0, 1]], 128, 1)
    red(v("GE"), v("T8"), A.add)
    ts(v("PMC"), v("GE"), -16.0, A.mult, 16.0, A.add)
    tt(v("PM"), v("PMC"), v("IP0"), A.add)
    ts(v("PML"), v("PM"), 11.0, A.min)
    ts(v("PLIN"), v("IOA"), v("PML"), A.add)
    qz("UQ", v("UT"))
    qz("XNQ", v("XN"))
    pickc(v("XQ"), v("XNQ"), v("PLIN"))
    act(v("XQS"), v("XNQS"), off=v("PLIN"))
    for e in (2, 3):
        ms(v("BT", e, 1536, 4), 0.0)
    for i in range(8):
        ms(v("POW", i, i + 1), 2.0 ** i)
    ms(v("WOUT"), 0.0)
    ms(v("TWO"), 2.0)
    ms(v("TWO", 7, 24, 8), 0.0)
    ms(v("ET"), 0.0)
    qz("LQ", v("ET"))
    node("v", lambda: g.vector.reciprocal(ap(v("INV")), ap(v("POW"))), [v("POW")], [v("INV")], 0.25)
    tt(v("T8B"), v("SEL8"), v("POW"), A.mult)
    red(v("WP"), v("T8B"), A.add)
    tt(v("T8C"), v("SEL8"), v("INV"), A.mult)
    red(v("IW"), v("T8C"), A.add)
    ms(v("CW"), 0.0)
    act(v("CW", 0, 512, 4), v("ONB"), v("WP"))
    qz("CWQ", v("CW"))
    asel(v("IM8"), v("INV"), [[-16, 8]], A.is_gt, 0.0, 0, 1)
    ms(v("MC"), 0.0)
    ts(v("IW2"), v("IW"), 0.5, A.mult)
    ts(v("FLA"), v("WI"), v("IW"), A.mult, -0.498, A.add)
    ts(v("FLB"), v("WI"), v("IW2"), A.mult, -0.498, A.add)
    ts(v("FLA"), v("FLA"), M23, A.add, M23, A.subtract)
    ts(v("FLC"), v("FLB"), M23, A.add, M23, A.subtract)
    ts(v("FLC"), v("FLC"), -2.0, A.mult)
    tt(v("FLB"), v("FLA"), v("FLC"), A.add)
    actl(v("NBT"), v("FLB"), -1.0, 1.0)
    act(v("MC", 0, 1024, 4), v("NBT"), v("WP"))
    act(v("MC", 1, 1024, 4), v("FLB"), v("WP"))
    ts(v("MC", 1024, 1056, 4), v("IM8"), v("WP"), A.mult)
    cp(v("MC", 1025, 1056, 4), v("SEL8"))
    qz("MCQ", v("MC"))
    ms(v("EB"), 0.0)
    for q, c in (("EHQ", 0.5), ("EBQ", 32.0)):
        for b in range(4):
            act(v("EB", 512 * b + b, 512 * b + 512, 4), v("ID"), c)
        qz(q, v("EB"))
    ms(v("TC"), 0.0)
    for e in range(4):
        act(v("TC", 512 * (e // 2) + e, 512 * (e // 2) + 512, 4), v("ID"))
    qz("TCQ", v("TC"))
    ms(v("NEG"), -1.0 / 512)
    ms(v("HI", 1520, 1536), 0.0)
    for n in ("EN0", "EN1", "KEEP", "Y3", "AJ", "Z16", "CI"):
        ms(v(n), 0.0)
    ms(v("ONE24"), 1.0)
    for n, w, f in (("D0R", 32, 15), ("D0L", 96, 0), ("D0G", 288, 0)):
        ms(v(n), 1.0)
        ms(v(n, f, w, 16), 0.0)
    ms(v("RST"), 0.0)
    ms(v("RST", 0, 48, 16), 2048.0)
    for k in range(8):
        iota(v("BASE", *qs(k)), [[2 ** (8 - k), 3]], 3 * (512 - 2 ** (9 - k)) - (1512 if k > 5 else 0))
    iota(v("NROW"), [[1, P]])
    iota(v("IOB"), [[16, 24]])
    iota(v("IOC"), [[4, 24]], 276)
    iota(v("IOD", 0, 18), [[16, 18]])
    ts(v("PADM"), v("QROW"), 12.0, A.is_ge, 1000.0, A.mult)
    ts(v("NRC"), v("PM"), 12.0, A.is_ge)
    ts(v("NRX"), v("NRC"), -5000.0, A.mult)
    ts(v("NRB"), v("NRC"), -100000.0, A.mult)
    ts(v("RST", 0, 48, 16), v("RST", 0, 48, 16), v("NRB"), A.add)
    ts(v("PADV"), v("QROW", 0, 48), 12.0, A.is_ge, 1024.0, A.mult)
    ts(v("MASK"), v("QROW"), v("PM"), A.is_equal)
    ts(v("NC"), v("IOB"), v("PM"), A.add)
    ts(v("N96"), v("NC"), 96.0, A.add)
    ts(v("N513"), v("NC"), 513.25, A.add)
    ts(v("JC"), v("IOA"), v("PM"), A.add, v("NRX"), A.add)
    ts(v("PADC"), v("IOC"), v("PM"), A.add, v("NRC"), A.mult)

    def seg(k):
        return 3 * (512 - 2 ** (9 - k))

    for t in range(R):
        u0 = (3 * t % 8) * 16
        for b in range(3):
            mm(b, 128, "XQ", 128 * b, "UQ", u0)
        mm(3, P, "UQ", u0, "XQ", 0)
        for b in range(3):
            ts(v("BJ", 8 * b, 8 * b + 8), ps(b, 128, 0, 16), 0.0, A.is_gt)
        scan(v("BW", 0, 24, 1, True), v("TWO", 0, 24, 1, True), v("BJ", 0, 24, 1, True), 0.0, A.mult, A.add)
        cp(v("WOUT", 0, 6, 2), v("BW", 0, 24, 8))
        lw = "LW%d" % t
        send("w", t, [(T[lw][:, 0:6], T.WOUT[:, 0:6])], [v("WOUT")] + ([v("LQ"), v("LQS")] if t == 0 else []), [v(lw)])
        for b in range(3):
            for q, k, n in ((6 * b, 0, 6), (18 + 2 * b, 6, 2)):
                act(v("BQO", q, q + n), v("BJ", 8 * b + k, 8 * b + k + n))
        ts(v("BT", 0, 1536, 4), ps(3, P), 0.0, A.is_gt)
        ts(v("BT", 1, 1536, 4), ps(3, P), 0.0, A.is_le)
        qz("BQ", v("BT"))
        mm(3, P, "CWQ", 0, "BQ", 0)
        wrow = len(nodes) - 1
        for b in range(3):
            mm(b, 272, "BQ", 128 * b, "MCQ", 0)
            act(v("XH", 256 * b, 256 * b + 256), ps(b, 256), 0.5)
            for q, k, n in ((6 * b, 0, 6), (18 + 2 * b, 6, 2)):
                tt(v("RIF", q, q + n), ps(b, n, 256 + k), v("BASE", q, q + n), A.add)
        cp(v("RI"), v("RIF"))
        tt(v("WR"), ps(3, P), v("PADM"), A.max)
        for h in range(2):
            ts(v("H%d" % h), v("WR"), v("IP%d" % h), A.is_equal, 0.5, A.subtract)
            scan(v("PA%d" % h, 0, P, 1, True), v("NEG"), v("H%d" % h, 0, P, 1, True), -0.5, A.add, A.max)
            scan(v("NX%d" % h, 0, P, 1, True), v("NEG"), v("H%d" % h, 0, P, 1, True), v("PA%d" % h, 0, 1), A.add, A.max)
            cp(v("NX%d" % h, P, P + 1), v("PA%d" % h, 0, 1))
            ts(v("DT", 2 * h, 1536, 4), v("NX%d" % h, 1, P + 1), M19, A.add, M19, A.subtract)
            tt(v("DT", 2 * h + 1, 1536, 4), v("NX%d" % h, 1, P + 1), v("DT", 2 * h, 1536, 4), A.subtract)
        qz("DQ", v("DT"))
        for b in range(3):
            mm(b, 256, "DQ", 128 * b, "TCQ", 0)
            actl(v("HI", 256 * b, 256 * b + 256), ps(b, 256), 512.0, 256.0)
        for b in range(4):
            mm(4 + b, P, "EHQ", 128 * b, "XQ", 0)
            nodes[-1]["behind"] = wrow
            act(v("FP", 768 * b, 768 * b + P), ps(4 + b, P))
            act(v("FP", 768 * b + P, 768 * b + 768), ps(4 + b, P))
        for b in range(3):
            cpg(v("XG", 16 * b, 16 * b + 16), v("XH", 256 * b, 256 * b + 256), v(lw, 2 * b, 2 * b + 1))
        ts(v("ZZ"), v("XG"), 0.0, A.is_equal, 1024.0, A.mult)
        tt(v("VV"), v("XG"), v("PADV"), A.add)
        tt(v("VV"), v("VV"), v("ZZ"), A.max)
        ts(v("DI"), v("XG"), 2.0, A.mult)
        for k in range(7):
            ts(v("XK", 48 * k, 48 * k + 48), v("DI"), 1 << k, A.bitwise_and)
        for k in range(8):
            vs, kl = ("VS", "KL") if k % 2 else ("VT2", "KL2")
            scan(v(vs), v("RST"), v("VV"), 4096.0, A.add, A.min)
            for b in range(3):
                if k < 7:
                    ts(v(kl, 16 * b, 16 * b + 16), v("XK", 48 * k + 16 * b, 48 * k + 16 * b + 16), v(vs, 16 * b + 15, 16 * b + 16), A.is_gt, 4096.0, A.mult)
            ts(v("KEEP", *qs(k)), v(vs, 15, 48, 16), float(1 << k), A.is_lt)
            if k < 7:
                tt(v("VV"), v("VV"), v(kl), A.max)
            if k in (KM, 5, 6):
                (lo, hi), s = ((0, 18) if k < 6 else (18, 24)), ("A" if k == KM else "B")
                tt(v("KB" + s, lo, hi), v("KEEP", lo, hi), v("BQO", lo, hi), A.mult)
                actl(v("M0" + s, lo, hi), v("KB" + s, lo, hi), -1.0, 1.0)
                tt(v("KU" + s, lo, hi), v("KB" + s, lo, hi), v("KEEP", lo, hi), A.subtract)
                actl(v("M1" + s, lo, hi), v("KU" + s, lo, hi), 1.0, 1.0)
            if k in (5, 7):
                lo, hi = (0, 18) if k < 6 else (18, 24)
                actl(v("DROP", lo, hi), v("KEEP", lo, hi), -1.0, 1.0)
                act(v("KQ", lo, hi), v("KEEP", lo, hi), 0.0625)
        for k in range(8):
            if k < 7:
                n, s0 = 2 ** (7 - k), seg(k)
                l_, h_ = ("LO2", "HH2") if k % 2 else ("LO", "HH")
                for b in range(3):
                    s, m = s0 + 2 * n * b, "A" if k <= KM else "B"
                    act(v(h_, n * b, n * b + n), v("HI", s + 1, s + 2 * n, 2), qc("M1" + m, k, b))
                    if k < KA:
                        act(v(l_, n * b, n * b + n), v("HI", s, s + 2 * n, 2), qc("M0" + m, k, b))
                    else:
                        ts(v(l_, n * b, n * b + n), v("HI", s, s + 2 * n, 2), qc("M0" + m, k, b), A.mult)
                tt(v("HI", seg(k + 1), seg(k + 1) + 3 * n), v(l_, 0, 3 * n), v(h_, 0, 3 * n), A.max)
            if k in (5, 7):
                h, lo, hi = (0, 0, 18) if k == 5 else (1, 18, 24)
                o, n = 16 * lo, 16 * (hi - lo)
                cpg(v("RG", o, o + n), v("HI", 1512 * h, 1512 + 24 * h), v("RI", lo, hi))
                tt(v("RMX", o, o + n), v("RG", o, o + n), v("MASK", 0, n), A.mult)
                scan(v("RSC", o, o + n), v("D0G", 0, n), v("RMX", o, o + n), 0.0, A.mult, A.max)
                tt(v("E1", lo, hi), v("RSC", o + 15, o + n, 16), v("DROP", lo, hi), A.mult)
                tt(v("EN%d" % h, 0, hi - lo), v("E1", lo, hi), v("KQ", lo, hi), A.subtract)
                tr(v("T1%d" % h), v("EN%d" % h))
                items = []
                for kk in (range(6) if h == 0 else (6, 7)):
                    gr = (3 * t + kk) % 8
                    for b in range(3):
                        p0, c0 = 32 * (gr // 2) + 8 * b, 16 * (gr % 2)
                        x = 6 * b + kk if h == 0 else 2 * b + kk - 6
                        items.append(("s" if (kk + b) % 2 else "a", T.Y3[p0:p0 + 8, c0:c0 + 16], T["T1%d" % h][x::32, 0:32], [v("T1%d" % h)], [v("Y3", c0, c0 + 16)]))
                dmas(items)
        tr(v("L3", 0, 32), v("Y3", 0, 32))
        e = v("L3", 0, 24)
        actl(v("EZ"), e, -4.01, 513.0, True)
        tt(v("EU0"), v("N513"), e, A.subtract)
        tt(v("EU"), v("EU0"), v("EZ"), A.subtract)
        cp(v("AL"), v("EU"))
        ts(v("FD"), v("Y3", 0, 32), 0.0, A.is_ge)
        scan(v("CI", 1, 33), v("D0R"), v("FD"), 0.0, A.mult, A.add)
        for h in range(2):
            last = v("CI", 16 * h + 15, 16 * h + 16)
            ts(v("Y3", 32 + 16 * h, 48 + 16 * h), v("CI", 16 * h, 16 * h + 16), last, A.subtract)
            actl(v("Y3", 64 + 16 * h, 80 + 16 * h), v("Z16"), 1.0, last)
        tr(v("L3", 32, 96), v("Y3", 32, 96))
        actl(v("BK"), e, -65536.0, 0.0, True)
        actl(v("BD"), v("BK"), -1.0, 4096.0)
        tt(v("JD"), v("JC"), v("BD"), A.add)
        scan(v("TS"), v("ONE24"), v("L3", 64, 88), 0.0, A.mult, A.add)
        tt(v("CD"), v("L3", 32, 56), v("TS"), A.add)
        ts(v("UU"), v("JD"), v("TS", 23, 24), A.add)
        tt(v("A1"), v("CD"), v("BK"), A.add)
        tt(v("A2"), v("UU"), v("CD"), A.subtract)
        tt(v("MNN"), v("A1"), v("A2"), A.min)
        tt(v("PO"), v("MNN"), v("PADC"), A.max)
        cp(v("PL"), v("PO"))
        scat(v("LWW"), v("PL"), v("NROW"))
        tt(v("LMK"), v("LWW", 0, K), v("MASK", 0, K), A.mult)
        scan(v("LSC"), v("D0L"), v("LMK"), 0.0, A.mult, A.add)
        cp(v("L6U"), v("LSC", 15, K, 16))
        for b in range(4):
            act(v("GZ", P * b, P * b + P), v("FP", 768 * b, 768 * b + 768), off=v("AL"))
            tt(v("TZ", 480 * b + K, 480 * b + 480), v("GZ", P * b, P * b + P), ps(4 + b, P), A.add)
        for b in range(4):
            z, o = v("TZ", 480 * b + K, 480 * b + 480), v("ET", b, 4 * K, 4)
            if b % 2:
                cpg(o, z, v("L6U"))
            else:
                act(o, z, off=v("L6U"))
        qz("EQ", v("ET"))
        send("e", t, [(T.LQ[:, 0:K].bitcast(dt.uint8), T.EQ[:, 0:K].bitcast(dt.uint8)), (T.LQS[:, 0:K], T.EQS[:, 0:K])],
             [v("EQ"), v("EQS")], [v("LQ", 0, K), v("LQS", 0, K)])
        ts(v("SA"), v("PO"), float(K), A.is_lt)
        tt(v("SB"), v("PO"), v("N96"), A.subtract)
        tt(v("SD"), v("SA"), v("SB"), A.mult)
        tt(v("SE"), v("SD"), v("N96"), A.add)
        cp(v("SL"), v("SE"))
        if t == R - 1:
            ts(v("AJA"), v("EU"), float(P), A.is_ge, -float(P), A.mult)
            tt(v("AJB"), v("EU"), v("AJA"), A.add)
            ts(v("AJC"), v("AJB"), M23, A.add, M23, A.subtract)
            ts(v("AJB"), v("AJC"), -7.5, A.add, 1.0 / 16, A.mult)
            ts(v("AJD"), v("AJB"), M23, A.add, M23, A.subtract)
            ts(v("AJA"), v("AJD"), -4.0, A.mult)
            tt(v("AJ", 0, 24), v("AJC"), v("AJA"), A.add)
            tr(v("AJT"), v("AJ"))
            ts(v("SC", 96, 192), v("LWW", 0, K), -7.5, A.add, 1.0 / 16, A.mult)
            ts(v("SC", 192, 288), v("SC", 96, 192), M23, A.add, M23, A.subtract)
            ts(v("SC", 288, 384), v("SC", 192, 288), -4.0, A.mult)
            tt(v("SC", 0, K), v("LWW", 0, K), v("SC", 288, 384), A.add)
            o = v("AJT")
            dmas([("s", T.al[:, C:C + K], T.SC[0:128:16, 0:K], [v("SC", 0, K)], [])]
                 + [("s", T.al[gr:gr + 1, 0:C], T[o[0]][32 * (gr // 2):32 * (gr // 2) + 24, o[1] + 16 * (gr % 2):o[1] + 16 * (gr % 2) + 12], [o], []) for gr in range(8)])
        if t == 0:
            qz("VQ", v("VT"))
            a, b = v("PLA", 0, 18), v("PLB", 0, 18)
            ts(a, v("IOD", 0, 18), v("PM"), A.add)
            ts(b, a, -5.5, A.add, 1.0 / 12, A.mult)
            ts(b, b, M23, A.add, M23, A.subtract)
            ts(b, b, 4.0, A.mult)
            tt(a, a, b, A.add)
            cp(v("PLOUT"), a)
        for b in range(4):
            mm(4 + b, 128, "WQ", 128 * b, "LQ", 0, True, False)
            mm(4 + b, 128, "EBQ", 128 * b, "LQ", 0, False, True)
        for b in range(4):
            o = v("TZ", 480 * b, 480 * b + K)
            if b % 2:
                ts(o, ps(4 + b, K), 0.03125, A.mult)
            else:
                act(o, ps(4 + b, K), 0.03125)
        for b in range(4):
            o, i = v("XT", b, 1536, 4), v("TZ", 480 * b, 480 * b + 480)
            if b % 2:
                cpg(o, i, v("SL"))
            else:
                act(o, i, off=v("SL"))
        qz("XQ", v("XT"))
    pickc(v("QC"), v("XQ"), v("PLOUT"))
    act(v("QCS"), v("XQS"), off=v("PLOUT"))
    mm(0, C, "VQ", 0, "QC", 0)
    dmas([("s", T.oc[:, :], T.QC[:, :].bitcast(dt.uint8), [v("QC")], [])])
    act(v("YO"), ps(0, C))
    dmas([("s" if k % 2 else "a", T.osc[4 * k:4 * k + 4, :], T.QCS[32 * k:32 * k + 4, :], [v("QCS")], []) for k in range(4)])
    dmas([("s", T.y[:, :], T.YO[:, :], [v("YO")], [])])

    n = len(nodes)
    pred = [dict() for _ in nodes]
    hist = {}
    for i, nw in enumerate(nodes):
        if "after" in nw:
            pred[i][nw["after"]] = True
        if "behind" in nw:
            pred[i][nw["behind"]] = False
        for kind, accs in (("r", nw["r"]), ("w", nw["w"])):
            for x in accs:
                for (k2, x2, j) in hist.get(x[0], ()):
                    od = nodes[j]
                    both = nw["kind"] == "d" and od["kind"] == "d"
                    if j == i or (both and (x[0] == "Y3" or od["tok"] == nw["tok"])):
                        continue
                    same = od["e"] == nw["e"] and od["kind"] == "c" and nw["kind"] == "c"
                    if (kind == "r" and k2 == "r" and (same or x[0][:3] != "PS.")) or not meet(x, x2):
                        continue
                    done = not (same and x[0][:3] == "PS." and nw["e"] == "p")
                    pred[i][j] = pred[i].get(j, False) or done
        for kind, accs in (("r", nw["r"]), ("w", nw["w"])):
            for x in accs:
                l = hist.setdefault(x[0], [])
                if kind == "w":
                    l[:] = [o for o in l if not covers(x, o[1]) or (nw["kind"] == "d" and nodes[o[2]]["kind"] == "d")]
                l.append((kind, x, i))
    succ = [[] for _ in nodes]
    left = [0] * n
    for i in range(n):
        left[i] = len(pred[i])
        for j in pred[i]:
            succ[j].append(i)
    path = [0.0] * n
    for i in range(n - 1, -1, -1):
        best = 0.0
        for j in succ[i]:
            best = max(best, path[j] + ((nodes[i]["lat"] + WAKE) if pred[j][i] else 0.0))
        path[i] = best + nodes[i]["dur"]
    free = {e: 0.0 for e in Q}
    est = [0.0] * n
    ready = {e: [] for e in list(Q) + [None]}
    for i in range(n):
        if not left[i]:
            ready[nodes[i]["e"]].append(i)
    order = []
    while len(order) < n:
        pick = None
        for e in ready:
            l = ready[e]
            if not l:
                continue
            f = free.get(e, 0.0)
            first = min(max(f, est[i]) for i in l)
            i = max((i for i in l if max(f, est[i]) <= first + DELTA), key=lambda i: path[i])
            s = max(f, est[i])
            if pick is None or s < pick[0]:
                pick = (s, i, e)
        s, i, e = pick
        ready[e].remove(i)
        order.append(i)
        end = s + nodes[i]["dur"]
        if e is not None:
            free[e] = end
        for j in succ[i]:
            w = end + nodes[i]["lat"] + (WAKE if nodes[j]["e"] is not None else 0.0) if pred[j][i] else s
            est[j] = max(est[j], w)
            left[j] -= 1
            if not left[j]:
                ready[nodes[j]["e"]].append(j)

    recs = {}
    for i in order:
        x = nodes[i]
        e, me = x["e"], (TOK.get(x["e"]) if x["kind"] == "c" else None)
        tok = me if x["kind"] == "c" else x["tok"]
        if e is not None:
            need = {}
            for kind, accs in (("r", x["r"]), ("w", x["w"])):
                for y in accs:
                    psum = y[0][:3] == "PS."
                    for (k2, y2, tk, cnt, snap) in recs.get(y[0], ()):
                        if kind == "r" and k2 == "r" and (tk == me or not psum):
                            continue
                        if x["kind"] == "d" and (tk == tok or tk[0] == "d" and y[0] == "Y3") or tk == me and psum and e == "p":
                            continue
                        if meet(y, y2) and know[e].get(tk, 0) < cnt and (tk not in need or need[tk][0] < cnt):
                            need[tk] = (cnt, snap)
            for tk in sorted(need, key=lambda q: (q == me, q)):
                cnt, snap = need[tk]
                if know[e].get(tk, 0) >= cnt or any(t2 != tk and s2[1].get(tk, 0) >= cnt and know[e].get(t2, 0) < s2[0] for t2, s2 in need.items()):
                    continue
                Q[e].wait_ge(T.sem[tk], cnt)
                for t3, c3 in list(snap.items()) + [(tk, cnt)]:
                    if know[e].get(t3, 0) < c3:
                        know[e][t3] = c3
        if x["kind"] == "c":
            total[tok] += 1
            x["fn"]().then_inc(T.sem[tok], 1)
            cnt = total[tok]
        else:
            cnt = x["cnt"]
            if x["kind"] == "d":
                x["fn"]().then_inc(T.sem[tok], 16)
            elif x["kind"] == "r":
                x["fn"]()
        snap = dict(know[e]) if e is not None else {}
        snap[tok] = cnt
        for kind, accs in (("r", x["r"]), ("w", x["w"])):
            for y in accs:
                l = recs.setdefault(y[0], [])
                if kind == "w":
                    l[:] = [o for o in l if not covers(y, o[1]) or (x["kind"] == "d" and o[2][0] == "d")]
                l.append((kind, y, tok, cnt, snap))
    for tok in sorted(total):
        if total[tok]:
            g.wait_ge(T.sem[tok], total[tok])
